import numpy as np
import ml_dtypes


def mxq(x, axis, fmt="e4m3"):
    dtype, down = {"e4m3": (ml_dtypes.float8_e4m3fn, 7), "e5m2": (ml_dtypes.float8_e5m2, 14)}[fmt]
    v = np.moveaxis(np.asarray(x, np.float32).astype(ml_dtypes.bfloat16).astype(np.float64), axis, -1)
    blocks = v.reshape(v.shape[:-1] + (-1, 32))
    amax = np.abs(blocks).max(-1, keepdims=True)
    byte = np.maximum(np.where(amax > 0, np.frexp(amax)[1] - 1 + 127, 0) - down, 1)
    scale = np.exp2(byte - 127.0)
    codes = (blocks / scale).astype(np.float32).astype(dtype).astype(np.float64)
    return np.moveaxis((codes * scale).reshape(v.shape), -1, axis)


WIDE = False


def mx_kscale(k):
    if not WIDE:
        return np.ones(k)
    levels = np.array([18, -18])
    if k % 512:
        return np.exp2(np.random.permutation(np.resize(levels, k // 32))).repeat(32)
    a = np.empty((k // 512, 16))
    for p in range(k // 512):
        a[p, :8] = np.random.permutation(np.resize(levels, 8))
        for g in range(8):
            far = levels[np.abs(levels - a[p, g]) >= 10]
            a[p, g + 8] = far[np.random.randint(len(far))]
    return np.exp2(a.ravel()).repeat(32)


def f64(x):
    return np.asarray(x).astype(np.float64)


def striped(idx):
    return np.tile(np.asarray(idx).reshape(-1, 16).T, (8, 1)).astype(np.uint16)


def unstriped(offs):
    return offs[:16].T.reshape(-1).astype(np.int64)

def planes(y):
    n, m = y.shape
    v = y.astype(np.float32).astype(ml_dtypes.bfloat16).astype(np.float64).reshape(n // 32, 32, m)
    top = np.abs(v).max(1)
    byte = np.clip(np.where(top > 0, np.frexp(top)[1] - 1 + 127 - 7, 1), 1, 254)
    codes = (v * np.exp2(127.0 - byte)[:, None, :]).reshape(n, m).astype(np.float32).astype(ml_dtypes.float8_e4m3fn).view(np.uint8)
    words = codes.reshape(n // 512, 128, 4, m).transpose(0, 1, 3, 2)
    return np.ascontiguousarray(words), np.ascontiguousarray(byte.astype(np.uint8).reshape(n // 512, 16, m))


N, C, D, R = 1024, 2048, 512, 512


def eight(codes):
    return np.concatenate([codes[h].reshape(-1, 16).T for h in range(8)]).astype(np.uint16)


def uneight(offs):
    return np.stack([offs[16 * h:16 * h + 16].T.reshape(-1) for h in range(8)]).astype(np.int64)


def setup_inputs():
    n = np.random.standard_normal
    s = mx_kscale(D)[:, None]
    u = mx_kscale(N)
    grid = lambda x: np.round(x * 32) / 32
    return {
        "xT": (n((D, R)) * (1.0 / np.sqrt(D)) * s).astype(np.float32),
        "cb": (grid(n((D, C))) / s).astype(np.float32),
        "norm": np.tile(np.random.randint(32, 129, N) / 64.0 / u, (128, 1)).astype(np.float32),
        "ts": np.tile(np.random.uniform(0.5, 1.5, N) * u, (128, 1)).astype(np.float32),
        "y": n((R, N)).astype(np.float32),
        "wt": (np.random.uniform(0.5, 1.5, (R, 1)) * 1.0 / np.sqrt(N)).astype(np.float32),
        "offs": eight(np.random.randint(0, C, (8, N))),
    }


def reference(xT, cb, norm, ts, y, wt, offs):
    code = uneight(offs)
    k = np.concatenate([f64(cb)[64 * h:64 * h + 64][:, code[h]] for h in range(8)]) * f64(norm)[:1]
    a = f64(ts)[:1] * (mxq(f64(xT), 0, "e4m3").T @ mxq(k, 0, "e4m3"))
    g = f64(wt) * np.minimum(np.maximum(a - f64(y), -1.0), 1.0)
    h = f64(ts)[:1] * g
    out_0 = mxq(h, 1, "e5m2") @ mxq(k, 1, "e4m3").T
    return (out_0,) + planes(out_0)

@@ -1,0 +1,254 @@
+from contextlib import ExitStack
+
+import concourse.mybir as mybir
+from concourse.masks import make_identity
+
+N, C, D, R = 1024, 2048, 512, 512
+FLOPS = 2 * 2 * R * N * D
+
+F32 = mybir.dt.float32
+BF16 = mybir.dt.bfloat16
+I32 = mybir.dt.int32
+U32 = mybir.dt.uint32
+U16 = mybir.dt.uint16
+U8 = mybir.dt.uint8
+E4M3 = mybir.dt.float8_e4m3fn_x4
+E5M2 = mybir.dt.float8_e5m2_x4
+ALU = mybir.AluOpType
+ACT = mybir.ActivationFunctionType
+
+P = 128
+LANES = 4
+PASS = P * LANES
+GROUPS = N // PASS
+
+
+def tile_attend_gpq_pl_hub_x_kernel(tc, xT, cb, norm, ts, y, wt, offs, out_0, out_1, out_2):
+    nc = tc.nc
+    with ExitStack() as ctx:
+        sb = ctx.enter_context(tc.tile_pool(name="sb", bufs=1))
+        ring = ctx.enter_context(tc.tile_pool(name="ring", bufs=3))
+        ps = ctx.enter_context(tc.psum_pool(name="ps", bufs=1))
+
+        def bank(b, shape):
+            return ps.tile(shape, F32, name="bank%d" % b)
+
+        def mx_tiles(name, width):
+            codes = sb.tile([P, width], U32, name=name + "_codes", align_bytes=64)
+            scales = sb.tile([P, width], U8, name=name + "_scales", align_bytes=64)
+            return codes, scales
+
+        def deal(engine_copy, dst, src):
+            engine_copy(dst.rearrange("p j s t -> p s t j"), src.rearrange("p t (s j) -> p s t j", j=LANES))
+
+        lists = sb.tile([P, N // 16], U16, name="lists")
+        nc.sync.dma_start(lists[:], offs)
+        norm_rows = sb.tile([P, N // P], F32, name="norm_rows")
+        nc.sync.dma_start(norm_rows[:], norm[0:1, :].rearrange("o (m c) -> (o m) c", m=P))
+        cb_planes = cb.rearrange("(p t) c -> p t c", t=LANES)
+        book = [sb.tile([P, C], F32, name="book%d" % t) for t in range(LANES)]
+        for t in range(LANES):
+            nc.sync.dma_start(book[t][:], cb_planes[:, t, :])
+        x_planes = xT.rearrange("(p t) r -> p t r", t=LANES)
+        x_raw = [sb.tile([P, LANES, R // 2], F32, name="x_raw%d" % a) for a in range(2)]
+        for a in range(2):
+            nc.sync.dma_start(x_raw[a][:], x_planes[:, :, a * (R // 2):(a + 1) * (R // 2)])
+        ts_col = sb.tile([P, GROUPS, LANES], F32, name="ts_col")
+        nc.sync.dma_start(ts_col[:], ts[0:1, :].rearrange("o (g s j) -> (o s) g j", g=GROUPS, j=LANES))
+        wt_col = sb.tile([P, LANES], F32, name="wt_col")
+        nc.sync.dma_start(wt_col[:], wt.rearrange("(p i) o -> p (i o)", i=LANES))
+        y_rows = y.rearrange("(p i) n -> p i n", i=LANES)
+        y_raw = {}
+        for g in range(GROUPS):
+            for i in range(LANES):
+                y_raw[g, i] = sb.tile([P, PASS], F32, name="y_raw%d%d" % (g, i))
+                nc.sync.dma_start(y_raw[g, i][:], y_rows[:, i, g * PASS:(g + 1) * PASS])
+
+        ident = sb.tile([P, P], F32, name="ident")
+        make_identity(nc, ident[:])
+
+        norm_all = sb.tile([P, N], F32, name="norm_all")
+        for half in range(2):
+            spread = bank(4 + half, [P, LANES, P])
+            for c in range(LANES):
+                col = half * LANES + c
+                nc.tensor.transpose(spread[:, c, :], norm_rows[:, col:col + 1].to_broadcast([P, P]), ident[:])
+            nc.scalar.copy(
+                norm_all[:].rearrange("p (m h c) -> p m h c", h=2, c=LANES)[:, :, half, :],
+                spread[:].rearrange("p c m -> p m c"))
+
+        k_f32 = {}
+        k_bf = [sb.tile([P, LANES, P, LANES], BF16, name="k_bf%d" % g, align_bytes=64) for g in range(GROUPS)]
+        for g in range(GROUPS):
+            for u in range(2):
+                k_f32[g, u] = sb.tile([P, 2, PASS], F32, name="k_f32_%d%d" % (g, u))
+
+        def round_k(g, u, engine_copy):
+            deal(engine_copy, k_bf[g][:, :, :, 2 * u:2 * u + 2], k_f32[g, u][:])
+
+        for t in range(LANES):
+            for g in range(GROUPS):
+                nc.vector.tensor_tensor(
+                    k_f32[g, t // 2][:, t % 2, :], book[t][:].indirect(lists[:, g * (PASS // 16):(g + 1) * (PASS // 16)]),
+                    norm_all[:, g * PASS:(g + 1) * PASS], ALU.mult)
+                if t == 1:
+                    round_k(g, 0, nc.scalar.copy)
+
+        ts_flat = ts_col[:].rearrange("p g j -> p (g j)")
+        ts_sq = sb.tile([P, GROUPS * LANES], F32, name="ts_sq")
+        nc.gpsimd.tensor_tensor(ts_sq[:], ts_flat, ts_flat, ALU.mult)
+        ts_hi = sb.tile([P, GROUPS * LANES], F32, name="ts_hi")
+        nc.scalar.activation(ts_hi[:], ts_flat, ACT.Abs)
+        ts_lo = sb.tile([P, GROUPS * LANES], F32, name="ts_lo")
+        nc.scalar.activation(ts_lo[:], ts_hi[:], ACT.Copy, scale=-1.0)
+        wt_all = bank(7, [P, R])
+        for i in range(LANES):
+            nc.tensor.transpose(wt_all[:, i * P:(i + 1) * P], wt_col[:, i:i + 1].to_broadcast([P, P]), ident[:])
+
+        kd, kn, kn_bf, clipped, h_bf, hq, y_turned, ts_y = {}, {}, {}, {}, {}, {}, {}, {}
+
+        def quantise_k_along_d(g):
+            kd[g] = mx_tiles("kd%d" % g, PASS)
+            nc.vector.quantize_mx(kd[g][0][:].bitcast(E4M3), kd[g][1][:], k_bf[g][:].rearrange("p j s t -> p (j s t)"))
+
+        def turn_k(g, u, b):
+            words = k_bf[g][:].rearrange("p j s t -> p (j s t)").bitcast(F32).rearrange("p (j s u) -> p j s u", j=LANES, u=2)
+            turned = bank(b, [P, LANES, P])
+            for j in range(LANES):
+                nc.tensor.transpose(turned[:, j, :], words[:, j, :, u], ident[:])
+            nc.scalar.copy(
+                kn_bf[g][:, :, u, :, :],
+                turned[:].rearrange("s j p -> s (j p)").bitcast(BF16).rearrange("s (j p e) -> s p e j", j=LANES, e=2))
+
+        def quantise_k_along_n(g):
+            kn[g] = mx_tiles("kn%d" % g, D)
+            nc.vector.quantize_mx(kn[g][0][:].bitcast(E4M3), kn[g][1][:], kn_bf[g][:].rearrange("s p u e j -> s (p u e j)"))
+
+        def turn_y(g, j, i):
+            if i == 0:
+                y_turned[g, j] = bank(j, [P, R])
+            nc.tensor.transpose(y_turned[g, j][:, i * P:(i + 1) * P], y_raw[g, i][:, j:PASS:LANES], ident[:])
+
+        def scale_y(g, j):
+            col = g * LANES + j
+            ts_y[g, j] = sb.tile([P, R], F32, name="ts_y%d" % col)
+            nc.scalar.activation(ts_y[g, j][:], y_turned[g, j][:], ACT.Copy, scale=ts_flat[:, col:col + 1])
+
+        def residual(g, j):
+            col = g * LANES + j
+            scores = bank((4, 5, 6, 4, 5, 4, 5, 4)[col], [P, R])
+            cols = slice(j * P, (j + 1) * P)
+            nc.tensor.matmul_mx(scores[:], kd[g][0][:, cols].bitcast(E4M3), kd[g][1][:, cols],
+                                x_codes[:].bitcast(E4M3), x_scales[:], start=True, stop=True)
+            diff = ring.tile([P, R], F32, name="diff")
+            nc.vector.scalar_tensor_tensor(diff[:], scores[:], ts_sq[:, col:col + 1], ts_y[g, j][:], ALU.mult, ALU.subtract)
+            return diff
+
+        def clip(g, j, diff):
+            col = g * LANES + j
+            nc.vector.tensor_scalar(clipped[g][:, j, :], diff[:], ts_hi[:, col:col + 1], ts_lo[:, col:col + 1], ALU.min, ALU.max)
+
+        def weigh(g, r0, r1):
+            quads = (r1 - r0) // LANES
+            nc.vector.tensor_tensor(
+                h_bf[g][:, r0:r1, :].rearrange("s (c q) j -> s c j q", q=LANES),
+                clipped[g][:, :, r0:r1].rearrange("s j (c q) -> s c j q", q=LANES),
+                wt_all[:, r0:r1].rearrange("s (c q) -> s c q", q=LANES).unsqueeze(2).to_broadcast([P, quads, LANES, LANES]),
+                ALU.mult)
+
+        def quantise_h(g, r0, r1):
+            nc.vector.quantize_mx(hq[g][0][:, r0:r1].bitcast(E5M2), hq[g][1][:, r0:r1],
+                                  h_bf[g][:, r0:r1, :].rearrange("s r j -> s (r j)"))
+
+        for g in range(GROUPS):
+            clipped[g] = sb.tile([P, LANES, R], F32, name="clipped%d" % g)
+            h_bf[g] = sb.tile([P, R, LANES], BF16, name="h_bf%d" % g, align_bytes=64)
+            hq[g] = mx_tiles("h%d" % g, R)
+            kn_bf[g] = sb.tile([P, P, 2, 2, LANES], BF16, name="kn_bf%d" % g, align_bytes=64)
+
+        x_bf = sb.tile([P, LANES, P, LANES], BF16, name="x_bf", align_bytes=64)
+        x_codes, x_scales = mx_tiles("x", R)
+        round_k(0, 1, nc.vector.tensor_copy)
+        deal(nc.scalar.copy, x_bf[:, :, 0:P // 2, :], x_raw[0][:])
+        round_k(1, 1, nc.scalar.copy)
+        deal(nc.vector.tensor_copy, x_bf[:, :, P // 2:P, :], x_raw[1][:])
+        quantise_k_along_d(0)
+        nc.vector.quantize_mx(x_codes[:].bitcast(E4M3), x_scales[:], x_bf[:].rearrange("p i m t -> p (i m t)"))
+        turn_k(0, 0, 6)
+        for i in range(LANES):
+            for j in range(LANES):
+                turn_y(0, j, i)
+        diffs = {}
+        for j in range(LANES):
+            scale_y(0, j)
+        for j in range(LANES):
+            diffs[j] = residual(0, j)
+            if j == 1:
+                quantise_k_along_d(1)
+            if j > 0:
+                clip(0, j - 1, diffs[j - 1])
+            if j == LANES - 1:
+                turn_k(0, 1, 3)
+            for i in range(LANES):
+                turn_y(1, j, i)
+            scale_y(1, j)
+        diffs[LANES] = residual(1, 0)
+        clip(0, LANES - 1, diffs[LANES - 1])
+        turn_k(1, 0, 6)
+        turn_k(1, 1, 6)
+        weigh(0, 0, R)
+        for j in range(1, LANES):
+            diffs[LANES + j] = residual(1, j)
+            clip(1, j - 1, diffs[LANES + j - 1])
+            if j == 1:
+                quantise_h(0, 0, R)
+            if j == 2:
+                quantise_k_along_n(0)
+        quantise_k_along_n(1)
+        clip(1, LANES - 1, diffs[2 * LANES - 1])
+
+        grad = [sb.tile([P, 2, D], F32, name="grad%d" % u) for u in range(2)]
+        grad_bf = sb.tile([P, D, LANES], BF16, name="grad_bf", align_bytes=64)
+        out_rows = out_0.rearrange("(p i) d -> p i d", i=LANES)
+        acc = {}
+        half = D // 2
+
+        def second_pass(i, g):
+            cols = slice(i * P, (i + 1) * P)
+            nc.tensor.matmul_mx(acc[i][:], hq[g][0][:, cols].bitcast(E5M2), hq[g][1][:, cols],
+                                kn[g][0][:].bitcast(E4M3), kn[g][1][:], start=(g == 0), stop=(g == GROUPS - 1))
+
+        def round_grad(engine_copy, u, cols):
+            engine_copy(
+                grad_bf[:, cols, 2 * u:2 * u + 2].rearrange("p (c q) i -> p c i q", q=LANES),
+                grad[u][:, :, cols].rearrange("p i (c q) -> p c i q", q=LANES))
+
+        for i in range(LANES):
+            acc[i] = bank(i, [P, D])
+            second_pass(i, 0)
+        weigh(1, 0, P)
+        for i in range(LANES):
+            if i + 1 < LANES:
+                weigh(1, (i + 1) * P, (i + 2) * P)
+            quantise_h(1, i * P, (i + 1) * P)
+            second_pass(i, 1)
+            for hh in range(2 if i == LANES - 1 else 1):
+                cols = slice(hh * half, (hh + 1) * half) if i == LANES - 1 else slice(0, D)
+                nc.scalar.copy(grad[i // 2][:, i % 2, cols], acc[i][:, cols])
+            nc.sync.dma_start(out_rows[:, i, :], grad[i // 2][:, i % 2, :])
+            if i == 1:
+                round_grad(nc.scalar.copy, 0, slice(0, D))
+
+        g_codes, g_scales = mx_tiles("grad", D)
+        words_out = out_1.rearrange("o p d b -> (o p) (d b)").bitcast(I32)
+        for hh in range(2):
+            round_grad(nc.vector.tensor_copy, 1, slice(hh * half, (hh + 1) * half))
+        for hh in range(2):
+            cols = slice(hh * half, (hh + 1) * half)
+            nc.vector.quantize_mx(g_codes[:, cols].bitcast(E4M3), g_scales[:, cols],
+                                  grad_bf[:, cols, :].rearrange("p d i -> p (d i)"))
+            nc.sync.dma_start(words_out[:, cols], g_codes[:, cols].bitcast(I32))
+        scales_out = out_2.rearrange("o f d -> (o f) d").bitcast(I32)
+        for q in range(4):
+            queue = (nc.sync, nc.scalar)[q % 2]
+            queue.dma_start(scales_out[4 * q:4 * q + 4, :], g_scales[32 * q:32 * q + 4, :].bitcast(I32))

@@ -146,7 +146,8 @@ def tile_attend_gpq_pl_hub_x_kernel(tc, xT, cb, norm, ts, y, wt, offs, out_0, ou
 
         def clip(g, j, diff):
             col = g * LANES + j
-            nc.vector.tensor_scalar(clipped[g][:, j, :], diff[:], ts_hi[:, col:col + 1], ts_lo[:, col:col + 1], ALU.min, ALU.max)
+            engine = nc.vector if col == GROUPS * LANES - 1 else nc.gpsimd
+            engine.tensor_scalar(clipped[g][:, j, :], diff[:], ts_hi[:, col:col + 1], ts_lo[:, col:col + 1], ALU.min, ALU.max)
 
         def weigh(g, r0, r1):
             quads = (r1 - r0) // LANES
@@ -168,19 +169,19 @@ def tile_attend_gpq_pl_hub_x_kernel(tc, xT, cb, norm, ts, y, wt, offs, out_0, ou
 
         x_bf = sb.tile([P, LANES, P, LANES], BF16, name="x_bf", align_bytes=64)
         x_codes, x_scales = mx_tiles("x", R)
-        round_k(0, 1, nc.vector.tensor_copy)
         deal(nc.scalar.copy, x_bf[:, :, 0:P // 2, :], x_raw[0][:])
-        round_k(1, 1, nc.scalar.copy)
+        round_k(0, 1, nc.scalar.copy)
         deal(nc.vector.tensor_copy, x_bf[:, :, P // 2:P, :], x_raw[1][:])
-        quantise_k_along_d(0)
+        round_k(1, 1, nc.scalar.copy)
         nc.vector.quantize_mx(x_codes[:].bitcast(E4M3), x_scales[:], x_bf[:].rearrange("p i m t -> p (i m t)"))
-        turn_k(0, 0, 6)
+        quantise_k_along_d(0)
         for i in range(LANES):
             for j in range(LANES):
                 turn_y(0, j, i)
         diffs = {}
         for j in range(LANES):
             scale_y(0, j)
+        turn_k(0, 0, 2)
         for j in range(LANES):
             diffs[j] = residual(0, j)
             if j == 1:
@@ -236,11 +237,10 @@ def tile_attend_gpq_pl_hub_x_kernel(tc, xT, cb, norm, ts, y, wt, offs, out_0, ou
                 cols = slice(hh * half, (hh + 1) * half) if i == LANES - 1 else slice(0, D)
                 nc.scalar.copy(grad[i // 2][:, i % 2, cols], acc[i][:, cols])
             nc.sync.dma_start(out_rows[:, i, :], grad[i // 2][:, i % 2, :])
-            if i == 1:
-                round_grad(nc.scalar.copy, 0, slice(0, D))
 
         g_codes, g_scales = mx_tiles("grad", D)
         words_out = out_1.rearrange("o p d b -> (o p) (d b)").bitcast(I32)
+        round_grad(nc.vector.tensor_copy, 0, slice(0, D))
         for hh in range(2):
             round_grad(nc.vector.tensor_copy, 1, slice(hh * half, (hh + 1) * half))
         for hh in range(2):

@@ -27,14 +27,14 @@ def tile_attend_gpq_pl_hub_x_kernel(tc, xT, cb, norm, ts, y, wt, offs, out_0, ou
     nc = tc.nc
     with ExitStack() as ctx:
         sb = ctx.enter_context(tc.tile_pool(name="sb", bufs=1))
-        ring = ctx.enter_context(tc.tile_pool(name="ring", bufs=3))
+        ring = ctx.enter_context(tc.tile_pool(name="ring", bufs=4))
         ps = ctx.enter_context(tc.psum_pool(name="ps", bufs=1))
 
         def bank(b, shape):
             return ps.tile(shape, F32, name="bank%d" % b)
 
-        def mx_tiles(name, width):
-            codes = sb.tile([P, width], U32, name=name + "_codes", align_bytes=64)
+        def mx_tiles(name, width, codes_tag=None):
+            codes = sb.tile([P, width], U32, name=name + "_codes", tag=codes_tag or name + "_codes", align_bytes=64)
             scales = sb.tile([P, width], U8, name=name + "_scales", align_bytes=64)
             return codes, scales
 
@@ -47,22 +47,24 @@ def tile_attend_gpq_pl_hub_x_kernel(tc, xT, cb, norm, ts, y, wt, offs, out_0, ou
         nc.sync.dma_start(norm_rows[:], norm[0:1, :].rearrange("o (m c) -> (o m) c", m=P))
         cb_planes = cb.rearrange("(p t) c -> p t c", t=LANES)
         book = [sb.tile([P, C], F32, name="book%d" % t) for t in range(LANES)]
-        for t in range(LANES):
-            nc.sync.dma_start(book[t][:], cb_planes[:, t, :])
         x_planes = xT.rearrange("(p t) r -> p t r", t=LANES)
-        x_raw = [sb.tile([P, LANES, R // 2], F32, name="x_raw%d" % a) for a in range(2)]
-        for a in range(2):
-            nc.sync.dma_start(x_raw[a][:], x_planes[:, :, a * (R // 2):(a + 1) * (R // 2)])
+        x_raw = [sb.tile([P, LANES, R // 2], F32, name="x_raw%d" % a, align_bytes=64) for a in range(2)]
+        for t in range(LANES):
+            if t == LANES - 1:
+                nc.sync.dma_start(x_raw[0][:], x_planes[:, :, 0:R // 2])
+            nc.sync.dma_start(book[t][:], cb_planes[:, t, :])
         ts_col = sb.tile([P, GROUPS, LANES], F32, name="ts_col")
-        nc.sync.dma_start(ts_col[:], ts[0:1, :].rearrange("o (g s j) -> (o s) g j", g=GROUPS, j=LANES))
+        nc.scalar.dma_start(ts_col[:], ts[0:1, :].rearrange("o (g s j) -> (o s) g j", g=GROUPS, j=LANES))
         wt_col = sb.tile([P, LANES], F32, name="wt_col")
-        nc.sync.dma_start(wt_col[:], wt.rearrange("(p i) o -> p (i o)", i=LANES))
+        nc.scalar.dma_start(wt_col[:], wt.rearrange("(p i) o -> p (i o)", i=LANES))
         y_rows = y.rearrange("(p i) n -> p i n", i=LANES)
         y_raw = {}
         for g in range(GROUPS):
             for i in range(LANES):
-                y_raw[g, i] = sb.tile([P, PASS], F32, name="y_raw%d%d" % (g, i))
+                y_raw[g, i] = sb.tile([P, PASS], F32, name="y_raw%d%d" % (g, i), align_bytes=64)
                 nc.sync.dma_start(y_raw[g, i][:], y_rows[:, i, g * PASS:(g + 1) * PASS])
+                if (g, i) == (0, 1):
+                    nc.sync.dma_start(x_raw[1][:], x_planes[:, :, R // 2:R])
 
         ident = sb.tile([P, P], F32, name="ident")
         make_identity(nc, ident[:])
@@ -78,10 +80,10 @@ def tile_attend_gpq_pl_hub_x_kernel(tc, xT, cb, norm, ts, y, wt, offs, out_0, ou
                 spread[:].rearrange("p c m -> p m c"))
 
         k_f32 = {}
-        k_bf = [sb.tile([P, LANES, P, LANES], BF16, name="k_bf%d" % g, align_bytes=64) for g in range(GROUPS)]
         for g in range(GROUPS):
             for u in range(2):
-                k_f32[g, u] = sb.tile([P, 2, PASS], F32, name="k_f32_%d%d" % (g, u))
+                k_f32[g, u] = sb.tile([P, 2, PASS], F32, name="k_f32_%d%d" % (g, u), align_bytes=64)
+        k_bf = [sb.tile([P, LANES, P, LANES], BF16, name="k_bf%d" % g, align_bytes=64) for g in range(GROUPS)]
 
         def round_k(g, u, engine_copy):
             deal(engine_copy, k_bf[g][:, :, :, 2 * u:2 * u + 2], k_f32[g, u][:])
@@ -101,18 +103,17 @@ def tile_attend_gpq_pl_hub_x_kernel(tc, xT, cb, norm, ts, y, wt, offs, out_0, ou
         nc.scalar.activation(ts_hi[:], ts_flat, ACT.Abs)
         ts_lo = sb.tile([P, GROUPS * LANES], F32, name="ts_lo")
         nc.scalar.activation(ts_lo[:], ts_hi[:], ACT.Copy, scale=-1.0)
-        wt_all = bank(7, [P, R])
-        for i in range(LANES):
-            nc.tensor.transpose(wt_all[:, i * P:(i + 1) * P], wt_col[:, i:i + 1].to_broadcast([P, P]), ident[:])
 
         kd, kn, kn_bf, clipped, h_bf, hq, y_turned, ts_y = {}, {}, {}, {}, {}, {}, {}, {}
 
         def quantise_k_along_d(g):
-            kd[g] = mx_tiles("kd%d" % g, PASS)
+            kd[g] = mx_tiles("kd%d" % g, PASS, ("x_raw1", "k_f32_00")[g])
             nc.vector.quantize_mx(kd[g][0][:].bitcast(E4M3), kd[g][1][:], k_bf[g][:].rearrange("p j s t -> p (j s t)"))
 
         def turn_k(g, u, b):
             words = k_bf[g][:].rearrange("p j s t -> p (j s t)").bitcast(F32).rearrange("p (j s u) -> p j s u", j=LANES, u=2)
+            if u == 0:
+                kn_bf[g] = sb.tile([P, P, 2, 2, LANES], BF16, name="kn_bf%d" % g, tag="kn_bf%d" % g, align_bytes=64)
             turned = bank(b, [P, LANES, P])
             for j in range(LANES):
                 nc.tensor.transpose(turned[:, j, :], words[:, j, :, u], ident[:])
@@ -126,17 +127,17 @@ def tile_attend_gpq_pl_hub_x_kernel(tc, xT, cb, norm, ts, y, wt, offs, out_0, ou
 
         def turn_y(g, j, i):
             if i == 0:
-                y_turned[g, j] = bank(j, [P, R])
+                y_turned[g, j] = bank((0, 1, 2, 3, 4, 5, 4, 6)[g * LANES + j], [P, R])
             nc.tensor.transpose(y_turned[g, j][:, i * P:(i + 1) * P], y_raw[g, i][:, j:PASS:LANES], ident[:])
 
         def scale_y(g, j):
             col = g * LANES + j
-            ts_y[g, j] = sb.tile([P, R], F32, name="ts_y%d" % col)
+            ts_y[g, j] = sb.tile([P, R], F32, name="ts_y%d" % col, align_bytes=64)
             nc.scalar.activation(ts_y[g, j][:], y_turned[g, j][:], ACT.Copy, scale=ts_flat[:, col:col + 1])
 
         def residual(g, j):
             col = g * LANES + j
-            scores = bank((4, 5, 6, 4, 5, 4, 5, 4)[col], [P, R])
+            scores = bank((col + LANES) % 8, [P, R])
             cols = slice(j * P, (j + 1) * P)
             nc.tensor.matmul_mx(scores[:], kd[g][0][:, cols].bitcast(E4M3), kd[g][1][:, cols],
                                 x_codes[:].bitcast(E4M3), x_scales[:], start=True, stop=True)
@@ -165,48 +166,44 @@ def tile_attend_gpq_pl_hub_x_kernel(tc, xT, cb, norm, ts, y, wt, offs, out_0, ou
             clipped[g] = sb.tile([P, LANES, R], F32, name="clipped%d" % g)
             h_bf[g] = sb.tile([P, R, LANES], BF16, name="h_bf%d" % g, align_bytes=64)
             hq[g] = mx_tiles("h%d" % g, R)
-            kn_bf[g] = sb.tile([P, P, 2, 2, LANES], BF16, name="kn_bf%d" % g, align_bytes=64)
+            pass
 
-        x_bf = sb.tile([P, LANES, P, LANES], BF16, name="x_bf", align_bytes=64)
+        x_bf = sb.tile([P, LANES, P, LANES], BF16, name="x_bf", tag="k_f32_00", align_bytes=64)
         x_codes, x_scales = mx_tiles("x", R)
         deal(nc.scalar.copy, x_bf[:, :, 0:P // 2, :], x_raw[0][:])
         round_k(0, 1, nc.scalar.copy)
-        deal(nc.vector.tensor_copy, x_bf[:, :, P // 2:P, :], x_raw[1][:])
         round_k(1, 1, nc.scalar.copy)
-        nc.vector.quantize_mx(x_codes[:].bitcast(E4M3), x_scales[:], x_bf[:].rearrange("p i m t -> p (i m t)"))
+        deal(nc.vector.tensor_copy, x_bf[:, :, P // 2:P, :], x_raw[1][:])
         quantise_k_along_d(0)
+        nc.vector.quantize_mx(x_codes[:].bitcast(E4M3), x_scales[:], x_bf[:].rearrange("p i m t -> p (i m t)"))
+        quantise_k_along_d(1)
         for i in range(LANES):
             for j in range(LANES):
                 turn_y(0, j, i)
-        diffs = {}
         for j in range(LANES):
             scale_y(0, j)
-        turn_k(0, 0, 2)
         for j in range(LANES):
-            diffs[j] = residual(0, j)
-            if j == 1:
-                quantise_k_along_d(1)
-            if j > 0:
-                clip(0, j - 1, diffs[j - 1])
-            if j == LANES - 1:
-                turn_k(0, 1, 3)
+            clip(0, j, residual(0, j))
+        wt_all = bank(7, [P, R])
+        for i in range(LANES):
+            nc.tensor.transpose(wt_all[:, i * P:(i + 1) * P], wt_col[:, i:i + 1].to_broadcast([P, P]), ident[:])
+        for j in range(LANES):
             for i in range(LANES):
                 turn_y(1, j, i)
             scale_y(1, j)
-        diffs[LANES] = residual(1, 0)
-        clip(0, LANES - 1, diffs[LANES - 1])
-        turn_k(1, 0, 6)
-        turn_k(1, 1, 6)
+            if j in (1, 2):
+                turn_k(0, j - 1, 7 - j)
+        turn_k(1, 0, 4)
+        turn_k(1, 1, 5)
+        clip(1, 0, residual(1, 0))
         weigh(0, 0, R)
-        for j in range(1, LANES):
-            diffs[LANES + j] = residual(1, j)
-            clip(1, j - 1, diffs[LANES + j - 1])
-            if j == 1:
-                quantise_h(0, 0, R)
-            if j == 2:
-                quantise_k_along_n(0)
+        clip(1, 1, residual(1, 1))
+        quantise_h(0, 0, R)
+        clip(1, 2, residual(1, 2))
+        quantise_k_along_n(0)
+        last = residual(1, 3)
         quantise_k_along_n(1)
-        clip(1, LANES - 1, diffs[2 * LANES - 1])
+        clip(1, 3, last)
 
         grad = [sb.tile([P, 2, D], F32, name="grad%d" % u) for u in range(2)]
         grad_bf = sb.tile([P, D, LANES], BF16, name="grad_bf", align_bytes=64)
@@ -241,8 +238,8 @@ def tile_attend_gpq_pl_hub_x_kernel(tc, xT, cb, norm, ts, y, wt, offs, out_0, ou
         g_codes, g_scales = mx_tiles("grad", D)
         words_out = out_1.rearrange("o p d b -> (o p) (d b)").bitcast(I32)
         round_grad(nc.vector.tensor_copy, 0, slice(0, D))
-        for hh in range(2):
-            round_grad(nc.vector.tensor_copy, 1, slice(hh * half, (hh + 1) * half))
+        round_grad(nc.vector.tensor_copy, 1, slice(0, half))
+        round_grad(nc.vector.tensor_copy, 1, slice(half, D))
         for hh in range(2):
             cols = slice(hh * half, (hh + 1) * half)
             nc.vector.quantize_mx(g_codes[:, cols].bitcast(E4M3), g_scales[:, cols],

@@ -27,7 +27,7 @@ def tile_attend_gpq_pl_hub_x_kernel(tc, xT, cb, norm, ts, y, wt, offs, out_0, ou
     nc = tc.nc
     with ExitStack() as ctx:
         sb = ctx.enter_context(tc.tile_pool(name="sb", bufs=1))
-        ring = ctx.enter_context(tc.tile_pool(name="ring", bufs=4))
+        laid = ctx.enter_context(tc.tile_pool(name="laid", bufs=1))
         ps = ctx.enter_context(tc.psum_pool(name="ps", bufs=1))
 
         def bank(b, shape):
@@ -49,6 +49,16 @@ def tile_attend_gpq_pl_hub_x_kernel(tc, xT, cb, norm, ts, y, wt, offs, out_0, ou
         book = [sb.tile([P, C], F32, name="book%d" % t) for t in range(LANES)]
         x_planes = xT.rearrange("(p t) r -> p t r", t=LANES)
         x_raw = [sb.tile([P, LANES, R // 2], F32, name="x_raw%d" % a, align_bytes=64) for a in range(2)]
+        y_rows = y.rearrange("(p i) n -> p i n", i=LANES)
+        y_raw = {}
+
+        def load_y(g, i):
+            if (g, i) == (0, LANES - 1):
+                y_raw[g, i] = laid.tile([P, PASS], F32, name="y_raw03", align_bytes=64, offset=3072)
+            else:
+                y_raw[g, i] = sb.tile([P, PASS], F32, name="y_raw%d%d" % (g, i), align_bytes=64)
+            nc.sync.dma_start(y_raw[g, i][:], y_rows[:, i, g * PASS:(g + 1) * PASS])
+
         for t in range(LANES):
             if t == LANES - 1:
                 nc.sync.dma_start(x_raw[0][:], x_planes[:, :, 0:R // 2])
@@ -57,12 +67,9 @@ def tile_attend_gpq_pl_hub_x_kernel(tc, xT, cb, norm, ts, y, wt, offs, out_0, ou
         nc.scalar.dma_start(ts_col[:], ts[0:1, :].rearrange("o (g s j) -> (o s) g j", g=GROUPS, j=LANES))
         wt_col = sb.tile([P, LANES], F32, name="wt_col")
         nc.scalar.dma_start(wt_col[:], wt.rearrange("(p i) o -> p (i o)", i=LANES))
-        y_rows = y.rearrange("(p i) n -> p i n", i=LANES)
-        y_raw = {}
         for g in range(GROUPS):
             for i in range(LANES):
-                y_raw[g, i] = sb.tile([P, PASS], F32, name="y_raw%d%d" % (g, i), align_bytes=64)
-                nc.sync.dma_start(y_raw[g, i][:], y_rows[:, i, g * PASS:(g + 1) * PASS])
+                load_y(g, i)
                 if (g, i) == (0, 1):
                     nc.sync.dma_start(x_raw[1][:], x_planes[:, :, R // 2:R])
 
@@ -78,6 +85,10 @@ def tile_attend_gpq_pl_hub_x_kernel(tc, xT, cb, norm, ts, y, wt, offs, out_0, ou
             nc.scalar.copy(
                 norm_all[:].rearrange("p (m h c) -> p m h c", h=2, c=LANES)[:, :, half, :],
                 spread[:].rearrange("p c m -> p m c"))
+
+        wt_all = bank(7, [P, R])
+        for i in range(LANES):
+            nc.tensor.transpose(wt_all[:, i * P:(i + 1) * P], wt_col[:, i:i + 1].to_broadcast([P, P]), ident[:])
 
         k_f32 = {}
         for g in range(GROUPS):
@@ -98,13 +109,13 @@ def tile_attend_gpq_pl_hub_x_kernel(tc, xT, cb, norm, ts, y, wt, offs, out_0, ou
 
         ts_flat = ts_col[:].rearrange("p g j -> p (g j)")
         ts_sq = sb.tile([P, GROUPS * LANES], F32, name="ts_sq")
-        nc.gpsimd.tensor_tensor(ts_sq[:], ts_flat, ts_flat, ALU.mult)
+        nc.scalar.activation(ts_sq[:], ts_flat, ACT.Square)
         ts_hi = sb.tile([P, GROUPS * LANES], F32, name="ts_hi")
         nc.scalar.activation(ts_hi[:], ts_flat, ACT.Abs)
         ts_lo = sb.tile([P, GROUPS * LANES], F32, name="ts_lo")
         nc.scalar.activation(ts_lo[:], ts_hi[:], ACT.Copy, scale=-1.0)
 
-        kd, kn, kn_bf, clipped, h_bf, hq, y_turned, ts_y = {}, {}, {}, {}, {}, {}, {}, {}
+        kd, kn, kn_bf, clipped, h_bf, hq, y_turned, ts_y, scores, k_turned = {}, {}, {}, {}, {}, {}, {}, {}, {}, {}
 
         def quantise_k_along_d(g):
             kd[g] = mx_tiles("kd%d" % g, PASS, ("x_raw1", "k_f32_00")[g])
@@ -112,43 +123,51 @@ def tile_attend_gpq_pl_hub_x_kernel(tc, xT, cb, norm, ts, y, wt, offs, out_0, ou
 
         def turn_k(g, u, b):
             words = k_bf[g][:].rearrange("p j s t -> p (j s t)").bitcast(F32).rearrange("p (j s u) -> p j s u", j=LANES, u=2)
-            if u == 0:
-                kn_bf[g] = sb.tile([P, P, 2, 2, LANES], BF16, name="kn_bf%d" % g, tag="kn_bf%d" % g, align_bytes=64)
-            turned = bank(b, [P, LANES, P])
+            k_turned[g, u] = bank(b, [P, LANES, P])
             for j in range(LANES):
-                nc.tensor.transpose(turned[:, j, :], words[:, j, :, u], ident[:])
+                nc.tensor.transpose(k_turned[g, u][:, j, :], words[:, j, :, u], ident[:])
+
+        def weave_k(g, u):
+            if u == 0:
+                kn_bf[g] = laid.tile([P, P, 2, 2, LANES], BF16, name="kn_bf%d" % g, align_bytes=64, offset=4096 * g)
             nc.scalar.copy(
                 kn_bf[g][:, :, u, :, :],
-                turned[:].rearrange("s j p -> s (j p)").bitcast(BF16).rearrange("s (j p e) -> s p e j", j=LANES, e=2))
+                k_turned[g, u][:].rearrange("s j p -> s (j p)").bitcast(BF16).rearrange("s (j p e) -> s p e j", j=LANES, e=2))
 
         def quantise_k_along_n(g):
-            kn[g] = mx_tiles("kn%d" % g, D)
+            kn[g] = mx_tiles("kn%d" % g, D, ("ts_y6", "ts_y7")[g])
             nc.vector.quantize_mx(kn[g][0][:].bitcast(E4M3), kn[g][1][:], kn_bf[g][:].rearrange("s p u e j -> s (p u e j)"))
 
         def turn_y(g, j, i):
             if i == 0:
-                y_turned[g, j] = bank((0, 1, 2, 3, 4, 5, 4, 6)[g * LANES + j], [P, R])
+                y_turned[g, j] = bank((0, 1, 2, 3, 2, 4, 5, 2)[g * LANES + j], [P, R])
             nc.tensor.transpose(y_turned[g, j][:, i * P:(i + 1) * P], y_raw[g, i][:, j:PASS:LANES], ident[:])
 
         def scale_y(g, j):
             col = g * LANES + j
-            ts_y[g, j] = sb.tile([P, R], F32, name="ts_y%d" % col, align_bytes=64)
-            nc.scalar.activation(ts_y[g, j][:], y_turned[g, j][:], ACT.Copy, scale=ts_flat[:, col:col + 1])
+            ts_y[g, j] = sb.tile([P, R], F32, name="ts_y%d" % col, align_bytes=64)[:]
+            nc.scalar.activation(ts_y[g, j], y_turned[g, j][:], ACT.Copy, scale=ts_flat[:, col:col + 1])
+
+        def score(g, j):
+            col = g * LANES + j
+            scores[g, j] = bank((6, 0, 1, 2, 3, 6, 0, 1)[col], [P, R])
+            cols = slice(j * P, (j + 1) * P)
+            nc.tensor.matmul_mx(scores[g, j][:], kd[g][0][:, cols].bitcast(E4M3), kd[g][1][:, cols],
+                                x_codes[:].bitcast(E4M3), x_scales[:], start=True, stop=True)
 
         def residual(g, j):
             col = g * LANES + j
-            scores = bank((col + LANES) % 8, [P, R])
-            cols = slice(j * P, (j + 1) * P)
-            nc.tensor.matmul_mx(scores[:], kd[g][0][:, cols].bitcast(E4M3), kd[g][1][:, cols],
-                                x_codes[:].bitcast(E4M3), x_scales[:], start=True, stop=True)
-            diff = ring.tile([P, R], F32, name="diff")
-            nc.vector.scalar_tensor_tensor(diff[:], scores[:], ts_sq[:, col:col + 1], ts_y[g, j][:], ALU.mult, ALU.subtract)
+            if g == 1:
+                diff = clipped[0][:, j, :]
+            else:
+                diff = sb.tile([P, R], F32, name="diff%d" % col)[:]
+            nc.vector.scalar_tensor_tensor(diff, scores[g, j][:], ts_sq[:, col:col + 1], ts_y[g, j], ALU.mult, ALU.subtract)
             return diff
 
         def clip(g, j, diff):
             col = g * LANES + j
-            engine = nc.vector if col == GROUPS * LANES - 1 else nc.gpsimd
-            engine.tensor_scalar(clipped[g][:, j, :], diff[:], ts_hi[:, col:col + 1], ts_lo[:, col:col + 1], ALU.min, ALU.max)
+            engine = nc.vector if j == LANES - 1 else nc.gpsimd
+            engine.tensor_scalar(clipped[g][:, j, :], diff, ts_hi[:, col:col + 1], ts_lo[:, col:col + 1], ALU.min, ALU.max)
 
         def weigh(g, r0, r1):
             quads = (r1 - r0) // LANES
@@ -166,10 +185,11 @@ def tile_attend_gpq_pl_hub_x_kernel(tc, xT, cb, norm, ts, y, wt, offs, out_0, ou
             clipped[g] = sb.tile([P, LANES, R], F32, name="clipped%d" % g)
             h_bf[g] = sb.tile([P, R, LANES], BF16, name="h_bf%d" % g, align_bytes=64)
             hq[g] = mx_tiles("h%d" % g, R)
-            pass
 
         x_bf = sb.tile([P, LANES, P, LANES], BF16, name="x_bf", tag="k_f32_00", align_bytes=64)
         x_codes, x_scales = mx_tiles("x", R)
+        turn_k(0, 0, 4)
+        turn_k(1, 0, 5)
         deal(nc.scalar.copy, x_bf[:, :, 0:P // 2, :], x_raw[0][:])
         round_k(0, 1, nc.scalar.copy)
         round_k(1, 1, nc.scalar.copy)
@@ -182,27 +202,29 @@ def tile_attend_gpq_pl_hub_x_kernel(tc, xT, cb, norm, ts, y, wt, offs, out_0, ou
                 turn_y(0, j, i)
         for j in range(LANES):
             scale_y(0, j)
+        weave_k(0, 0)
+        weave_k(1, 0)
         for j in range(LANES):
+            score(0, j)
             clip(0, j, residual(0, j))
-        wt_all = bank(7, [P, R])
-        for i in range(LANES):
-            nc.tensor.transpose(wt_all[:, i * P:(i + 1) * P], wt_col[:, i:i + 1].to_broadcast([P, P]), ident[:])
+        for j in range(LANES):
+            score(1, j)
         for j in range(LANES):
             for i in range(LANES):
                 turn_y(1, j, i)
             scale_y(1, j)
-            if j in (1, 2):
-                turn_k(0, j - 1, 7 - j)
-        turn_k(1, 0, 4)
-        turn_k(1, 1, 5)
+        for g in range(GROUPS):
+            turn_k(g, 1, 4 + g)
+            weave_k(g, 1)
+        weigh(0, 0, R // 2)
+        weigh(0, R // 2, R)
+        quantise_h(0, 0, R // 2)
         clip(1, 0, residual(1, 0))
-        weigh(0, 0, R)
+        quantise_h(0, R // 2, R)
         clip(1, 1, residual(1, 1))
-        quantise_h(0, 0, R)
         clip(1, 2, residual(1, 2))
-        quantise_k_along_n(0)
         last = residual(1, 3)
-        quantise_k_along_n(1)
+        quantise_k_along_n(0)
         clip(1, 3, last)
 
         grad = [sb.tile([P, 2, D], F32, name="grad%d" % u) for u in range(2)]
@@ -222,12 +244,14 @@ def tile_attend_gpq_pl_hub_x_kernel(tc, xT, cb, norm, ts, y, wt, offs, out_0, ou
                 grad[u][:, :, cols].rearrange("p i (c q) -> p c i q", q=LANES))
 
         for i in range(LANES):
-            acc[i] = bank(i, [P, D])
+            acc[i] = bank((3, 6, 0, 1)[i], [P, D])
             second_pass(i, 0)
         weigh(1, 0, P)
         for i in range(LANES):
             if i + 1 < LANES:
                 weigh(1, (i + 1) * P, (i + 2) * P)
+            if i == 0:
+                quantise_k_along_n(1)
             quantise_h(1, i * P, (i + 1) * P)
             second_pass(i, 1)
             for hh in range(2 if i == LANES - 1 else 1):

@@ -43,8 +43,8 @@ def tile_attend_gpq_pl_hub_x_kernel(tc, xT, cb, norm, ts, y, wt, offs, out_0, ou
 
         lists = sb.tile([P, N // 16], U16, name="lists")
         nc.sync.dma_start(lists[:], offs)
-        norm_rows = sb.tile([P, N // P], F32, name="norm_rows")
-        nc.sync.dma_start(norm_rows[:], norm[0:1, :].rearrange("o (m c) -> (o m) c", m=P))
+        norm_col = sb.tile([P, GROUPS, LANES], F32, name="norm_col")
+        nc.sync.dma_start(norm_col[:], norm[0:1, :].rearrange("o (g m c) -> (o m) g c", g=GROUPS, c=LANES))
         cb_planes = cb.rearrange("(p t) c -> p t c", t=LANES)
         book = [sb.tile([P, C], F32, name="book%d" % t) for t in range(LANES)]
         x_planes = xT.rearrange("(p t) r -> p t r", t=LANES)
@@ -76,15 +76,12 @@ def tile_attend_gpq_pl_hub_x_kernel(tc, xT, cb, norm, ts, y, wt, offs, out_0, ou
         ident = sb.tile([P, P], F32, name="ident")
         make_identity(nc, ident[:])
 
-        norm_all = sb.tile([P, N], F32, name="norm_all")
-        for half in range(2):
-            spread = bank(4 + half, [P, LANES, P])
+        norm_all = [sb.tile([P, PASS], F32, name="norm_all%d" % g) for g in range(GROUPS)]
+        for g in range(GROUPS):
+            spread = bank(4 + g, [P, LANES, P])
             for c in range(LANES):
-                col = half * LANES + c
-                nc.tensor.transpose(spread[:, c, :], norm_rows[:, col:col + 1].to_broadcast([P, P]), ident[:])
-            nc.scalar.copy(
-                norm_all[:].rearrange("p (m h c) -> p m h c", h=2, c=LANES)[:, :, half, :],
-                spread[:].rearrange("p c m -> p m c"))
+                nc.tensor.transpose(spread[:, c, :], norm_col[:, g, c:c + 1].to_broadcast([P, P]), ident[:])
+            nc.scalar.copy(norm_all[g][:].rearrange("p (m c) -> p m c", c=LANES), spread[:].rearrange("p c m -> p m c"))
 
         wt_all = bank(7, [P, R])
         for i in range(LANES):
@@ -96,16 +93,24 @@ def tile_attend_gpq_pl_hub_x_kernel(tc, xT, cb, norm, ts, y, wt, offs, out_0, ou
                 k_f32[g, u] = sb.tile([P, 2, PASS], F32, name="k_f32_%d%d" % (g, u), align_bytes=64)
         k_bf = [sb.tile([P, LANES, P, LANES], BF16, name="k_bf%d" % g, align_bytes=64) for g in range(GROUPS)]
 
-        def round_k(g, u, engine_copy):
-            deal(engine_copy, k_bf[g][:, :, :, 2 * u:2 * u + 2], k_f32[g, u][:])
+        def round_k(g, u, n0, n1):
+            deal(nc.scalar.copy, k_bf[g][:, :, n0 // LANES:n1 // LANES, 2 * u:2 * u + 2], k_f32[g, u][:, :, n0:n1])
+
+        def gather(t, g, n0, n1):
+            first = g * PASS
+            nc.vector.tensor_tensor(
+                k_f32[g, t // 2][:, t % 2, n0:n1], book[t][:].indirect(lists[:, (first + n0) // 16:(first + n1) // 16]),
+                norm_all[g][:, n0:n1], ALU.mult)
 
         for t in range(LANES):
             for g in range(GROUPS):
-                nc.vector.tensor_tensor(
-                    k_f32[g, t // 2][:, t % 2, :], book[t][:].indirect(lists[:, g * (PASS // 16):(g + 1) * (PASS // 16)]),
-                    norm_all[:, g * PASS:(g + 1) * PASS], ALU.mult)
+                if (t, g) == (LANES - 1, 0):
+                    gather(t, g, 0, PASS // 2)
+                    gather(t, g, PASS // 2, PASS)
+                else:
+                    gather(t, g, 0, PASS)
                 if t == 1:
-                    round_k(g, 0, nc.scalar.copy)
+                    round_k(g, 0, 0, PASS)
 
         ts_flat = ts_col[:].rearrange("p g j -> p (g j)")
         ts_sq = sb.tile([P, GROUPS * LANES], F32, name="ts_sq")
@@ -135,12 +140,12 @@ def tile_attend_gpq_pl_hub_x_kernel(tc, xT, cb, norm, ts, y, wt, offs, out_0, ou
                 k_turned[g, u][:].rearrange("s j p -> s (j p)").bitcast(BF16).rearrange("s (j p e) -> s p e j", j=LANES, e=2))
 
         def quantise_k_along_n(g):
-            kn[g] = mx_tiles("kn%d" % g, D, ("ts_y6", "ts_y7")[g])
+            kn[g] = mx_tiles("kn%d" % g, D, ("diff3", "ts_y7")[g])
             nc.vector.quantize_mx(kn[g][0][:].bitcast(E4M3), kn[g][1][:], kn_bf[g][:].rearrange("s p u e j -> s (p u e j)"))
 
         def turn_y(g, j, i):
             if i == 0:
-                y_turned[g, j] = bank((0, 1, 2, 3, 2, 4, 5, 2)[g * LANES + j], [P, R])
+                y_turned[g, j] = bank((0, 1, 2, 3, 4, 5, 2, 4)[g * LANES + j], [P, R])
             nc.tensor.transpose(y_turned[g, j][:, i * P:(i + 1) * P], y_raw[g, i][:, j:PASS:LANES], ident[:])
 
         def scale_y(g, j):
@@ -160,13 +165,13 @@ def tile_attend_gpq_pl_hub_x_kernel(tc, xT, cb, norm, ts, y, wt, offs, out_0, ou
             if g == 1:
                 diff = clipped[0][:, j, :]
             else:
-                diff = sb.tile([P, R], F32, name="diff%d" % col)[:]
+                diff = sb.tile([P, R], F32, name="diff%d" % col, align_bytes=64)[:]
             nc.vector.scalar_tensor_tensor(diff, scores[g, j][:], ts_sq[:, col:col + 1], ts_y[g, j], ALU.mult, ALU.subtract)
             return diff
 
         def clip(g, j, diff):
             col = g * LANES + j
-            engine = nc.vector if j == LANES - 1 else nc.gpsimd
+            engine = nc.vector if j >= 2 else nc.gpsimd
             engine.tensor_scalar(clipped[g][:, j, :], diff, ts_hi[:, col:col + 1], ts_lo[:, col:col + 1], ALU.min, ALU.max)
 
         def weigh(g, r0, r1):
@@ -191,8 +196,9 @@ def tile_attend_gpq_pl_hub_x_kernel(tc, xT, cb, norm, ts, y, wt, offs, out_0, ou
         turn_k(0, 0, 4)
         turn_k(1, 0, 5)
         deal(nc.scalar.copy, x_bf[:, :, 0:P // 2, :], x_raw[0][:])
-        round_k(0, 1, nc.scalar.copy)
-        round_k(1, 1, nc.scalar.copy)
+        round_k(0, 1, 0, PASS // 2)
+        round_k(0, 1, PASS // 2, PASS)
+        round_k(1, 1, 0, PASS)
         deal(nc.vector.tensor_copy, x_bf[:, :, P // 2:P, :], x_raw[1][:])
         quantise_k_along_d(0)
         nc.vector.quantize_mx(x_codes[:].bitcast(E4M3), x_scales[:], x_bf[:].rearrange("p i m t -> p (i m t)"))
@@ -204,28 +210,31 @@ def tile_attend_gpq_pl_hub_x_kernel(tc, xT, cb, norm, ts, y, wt, offs, out_0, ou
             scale_y(0, j)
         weave_k(0, 0)
         weave_k(1, 0)
+        diffs = {}
         for j in range(LANES):
             score(0, j)
-            clip(0, j, residual(0, j))
+            diffs[0, j] = residual(0, j)
+        for j in range(LANES):
+            clip(0, j, diffs[0, j])
         for j in range(LANES):
             score(1, j)
+        turn_k(0, 1, 2)
+        weave_k(0, 1)
         for j in range(LANES):
             for i in range(LANES):
                 turn_y(1, j, i)
             scale_y(1, j)
-        for g in range(GROUPS):
-            turn_k(g, 1, 4 + g)
-            weave_k(g, 1)
+        turn_k(1, 1, 5)
+        weave_k(1, 1)
         weigh(0, 0, R // 2)
         weigh(0, R // 2, R)
         quantise_h(0, 0, R // 2)
-        clip(1, 0, residual(1, 0))
-        quantise_h(0, R // 2, R)
-        clip(1, 1, residual(1, 1))
-        clip(1, 2, residual(1, 2))
-        last = residual(1, 3)
         quantise_k_along_n(0)
-        clip(1, 3, last)
+        quantise_h(0, R // 2, R)
+        for j in range(LANES):
+            diffs[1, j] = residual(1, j)
+        for j in range(LANES):
+            clip(1, j, diffs[1, j])
 
         grad = [sb.tile([P, 2, D], F32, name="grad%d" % u) for u in range(2)]
         grad_bf = sb.tile([P, D, LANES], BF16, name="grad_bf", align_bytes=64)

@@ -53,10 +53,7 @@ def tile_attend_gpq_pl_hub_x_kernel(tc, xT, cb, norm, ts, y, wt, offs, out_0, ou
         y_raw = {}
 
         def load_y(g, i):
-            if (g, i) == (0, LANES - 1):
-                y_raw[g, i] = laid.tile([P, PASS], F32, name="y_raw03", align_bytes=64, offset=3072)
-            else:
-                y_raw[g, i] = sb.tile([P, PASS], F32, name="y_raw%d%d" % (g, i), align_bytes=64)
+            y_raw[g, i] = sb.tile([P, PASS], F32, name="y_raw%d%d" % (g, i), align_bytes=64)
             nc.sync.dma_start(y_raw[g, i][:], y_rows[:, i, g * PASS:(g + 1) * PASS])
 
         for t in range(LANES):
@@ -120,7 +117,7 @@ def tile_attend_gpq_pl_hub_x_kernel(tc, xT, cb, norm, ts, y, wt, offs, out_0, ou
         ts_lo = sb.tile([P, GROUPS * LANES], F32, name="ts_lo")
         nc.scalar.activation(ts_lo[:], ts_hi[:], ACT.Copy, scale=-1.0)
 
-        kd, kn, kn_bf, clipped, h_bf, hq, y_turned, ts_y, scores, k_turned = {}, {}, {}, {}, {}, {}, {}, {}, {}, {}
+        kd, kn, kn_bf, clipped, h_bf, hq, y_turned, ts_y, scores, k_turned, y_dealt = {}, {}, {}, {}, {}, {}, {}, {}, {}, {}, {}
 
         def quantise_k_along_d(g):
             kd[g] = mx_tiles("kd%d" % g, PASS, ("x_raw1", "k_f32_00")[g])
@@ -146,7 +143,20 @@ def tile_attend_gpq_pl_hub_x_kernel(tc, xT, cb, norm, ts, y, wt, offs, out_0, ou
         def turn_y(g, j, i):
             if i == 0:
                 y_turned[g, j] = bank((0, 1, 2, 3, 4, 5, 2, 4)[g * LANES + j], [P, R])
-            nc.tensor.transpose(y_turned[g, j][:, i * P:(i + 1) * P], y_raw[g, i][:, j:PASS:LANES], ident[:])
+            cols = y_dealt[g, i][:, j, :] if (g, i) in y_dealt else y_raw[g, i][:, j:PASS:LANES]
+            nc.tensor.transpose(y_turned[g, j][:, i * P:(i + 1) * P], cols, ident[:])
+
+        def deal_y(g, i, on_vector):
+            if g == 0:
+                y_dealt[g, i] = laid.tile([P, LANES, P], F32, name="y_dealt0", align_bytes=64, offset=3072)
+            else:
+                y_dealt[g, i] = sb.tile([P, LANES, P], F32, name="y_dealt1", align_bytes=64)
+            dst = y_dealt[g, i][:].rearrange("p j (c q) -> p c j q", q=LANES)
+            src = y_raw[g, i][:].rearrange("p (c q j) -> p c j q", q=LANES, j=LANES)
+            if on_vector:
+                nc.vector.tensor_copy(dst, src)
+            else:
+                nc.gpsimd.tensor_scalar(dst, src, 1.0, 0.0, ALU.mult, ALU.add)
 
         def scale_y(g, j):
             col = g * LANES + j
@@ -201,6 +211,7 @@ def tile_attend_gpq_pl_hub_x_kernel(tc, xT, cb, norm, ts, y, wt, offs, out_0, ou
         round_k(1, 1, 0, PASS)
         deal(nc.vector.tensor_copy, x_bf[:, :, P // 2:P, :], x_raw[1][:])
         quantise_k_along_d(0)
+        deal_y(0, LANES - 1, True)
         nc.vector.quantize_mx(x_codes[:].bitcast(E4M3), x_scales[:], x_bf[:].rearrange("p i m t -> p (i m t)"))
         quantise_k_along_d(1)
         for i in range(LANES):
@@ -211,6 +222,7 @@ def tile_attend_gpq_pl_hub_x_kernel(tc, xT, cb, norm, ts, y, wt, offs, out_0, ou
         weave_k(0, 0)
         weave_k(1, 0)
         diffs = {}
+        deal_y(1, LANES - 1, False)
         for j in range(LANES):
             score(0, j)
             diffs[0, j] = residual(0, j)

@@ -53,12 +53,13 @@ def tile_attend_gpq_pl_hub_x_kernel(tc, xT, cb, norm, ts, y, wt, offs, out_0, ou
         y_raw = {}
 
         def load_y(g, i):
-            y_raw[g, i] = sb.tile([P, PASS], F32, name="y_raw%d%d" % (g, i), align_bytes=64)
+            if (g, i) == (0, LANES - 1):
+                y_raw[g, i] = laid.tile([P, PASS], F32, name="y_raw03", align_bytes=64, offset=3072)
+            else:
+                y_raw[g, i] = sb.tile([P, PASS], F32, name="y_raw%d%d" % (g, i), align_bytes=64)
             nc.sync.dma_start(y_raw[g, i][:], y_rows[:, i, g * PASS:(g + 1) * PASS])
 
         for t in range(LANES):
-            if t == LANES - 1:
-                nc.sync.dma_start(x_raw[0][:], x_planes[:, :, 0:R // 2])
             nc.sync.dma_start(book[t][:], cb_planes[:, t, :])
         ts_col = sb.tile([P, GROUPS, LANES], F32, name="ts_col")
         nc.scalar.dma_start(ts_col[:], ts[0:1, :].rearrange("o (g s j) -> (o s) g j", g=GROUPS, j=LANES))
@@ -68,7 +69,8 @@ def tile_attend_gpq_pl_hub_x_kernel(tc, xT, cb, norm, ts, y, wt, offs, out_0, ou
             for i in range(LANES):
                 load_y(g, i)
                 if (g, i) == (0, 1):
-                    nc.sync.dma_start(x_raw[1][:], x_planes[:, :, R // 2:R])
+                    for a in range(2):
+                        nc.sync.dma_start(x_raw[a][:], x_planes[:, :, a * (R // 2):(a + 1) * (R // 2)])
 
         ident = sb.tile([P, P], F32, name="ident")
         make_identity(nc, ident[:])
@@ -78,7 +80,7 @@ def tile_attend_gpq_pl_hub_x_kernel(tc, xT, cb, norm, ts, y, wt, offs, out_0, ou
             spread = bank(4 + g, [P, LANES, P])
             for c in range(LANES):
                 nc.tensor.transpose(spread[:, c, :], norm_col[:, g, c:c + 1].to_broadcast([P, P]), ident[:])
-            nc.scalar.copy(norm_all[g][:].rearrange("p (m c) -> p m c", c=LANES), spread[:].rearrange("p c m -> p m c"))
+            (nc.scalar.copy, nc.vector.tensor_copy)[g](norm_all[g][:].rearrange("p (m c) -> p m c", c=LANES), spread[:].rearrange("p c m -> p m c"))
 
         wt_all = bank(7, [P, R])
         for i in range(LANES):
@@ -146,17 +148,11 @@ def tile_attend_gpq_pl_hub_x_kernel(tc, xT, cb, norm, ts, y, wt, offs, out_0, ou
             cols = y_dealt[g, i][:, j, :] if (g, i) in y_dealt else y_raw[g, i][:, j:PASS:LANES]
             nc.tensor.transpose(y_turned[g, j][:, i * P:(i + 1) * P], cols, ident[:])
 
-        def deal_y(g, i, on_vector):
-            if g == 0:
-                y_dealt[g, i] = laid.tile([P, LANES, P], F32, name="y_dealt0", align_bytes=64, offset=3072)
-            else:
-                y_dealt[g, i] = sb.tile([P, LANES, P], F32, name="y_dealt1", align_bytes=64)
-            dst = y_dealt[g, i][:].rearrange("p j (c q) -> p c j q", q=LANES)
-            src = y_raw[g, i][:].rearrange("p (c q j) -> p c j q", q=LANES, j=LANES)
-            if on_vector:
-                nc.vector.tensor_copy(dst, src)
-            else:
-                nc.gpsimd.tensor_scalar(dst, src, 1.0, 0.0, ALU.mult, ALU.add)
+        def deal_y(g, i):
+            y_dealt[g, i] = laid.tile([P, LANES, P], F32, name="y_dealt%d" % i, align_bytes=64, offset=8192 + 2048 * (i - 2))
+            nc.gpsimd.tensor_scalar(y_dealt[g, i][:].rearrange("p j (c q) -> p c j q", q=LANES),
+                                    y_raw[g, i][:].rearrange("p (c q j) -> p c j q", q=LANES, j=LANES),
+                                    1.0, 0.0, ALU.mult, ALU.add)
 
         def scale_y(g, j):
             col = g * LANES + j
@@ -174,6 +170,8 @@ def tile_attend_gpq_pl_hub_x_kernel(tc, xT, cb, norm, ts, y, wt, offs, out_0, ou
             col = g * LANES + j
             if g == 1:
                 diff = clipped[0][:, j, :]
+            elif j == 2:
+                diff = laid.tile([P, R], F32, name="diff2", align_bytes=64, offset=8192 + 1024)[:]
             else:
                 diff = sb.tile([P, R], F32, name="diff%d" % col, align_bytes=64)[:]
             nc.vector.scalar_tensor_tensor(diff, scores[g, j][:], ts_sq[:, col:col + 1], ts_y[g, j], ALU.mult, ALU.subtract)
@@ -182,36 +180,46 @@ def tile_attend_gpq_pl_hub_x_kernel(tc, xT, cb, norm, ts, y, wt, offs, out_0, ou
         def clip(g, j, diff):
             col = g * LANES + j
             engine = nc.vector if j >= 2 else nc.gpsimd
-            engine.tensor_scalar(clipped[g][:, j, :], diff, ts_hi[:, col:col + 1], ts_lo[:, col:col + 1], ALU.min, ALU.max)
+            pieces = (slice(0, R // 2), slice(R // 2, R)) if j == LANES - 1 else (slice(0, R),)
+            for rows in pieces:
+                engine.tensor_scalar(clipped[g][:, j, rows], diff[:, rows], ts_hi[:, col:col + 1], ts_lo[:, col:col + 1],
+                                     ALU.min, ALU.max)
 
-        def weigh(g, r0, r1):
-            quads = (r1 - r0) // LANES
+        def weigh(g, r0, r1, tile_first=None):
+            pairs = (r1 - r0) // 2
+            first = r0 if tile_first is None else tile_first
+            width = R // 2 if g == 0 else P
+            if first == r0:
+                if (g, r0) == (1, P):
+                    h_bf[g, r0] = laid.tile([P, width, LANES], BF16, name="h_bf_laid", align_bytes=64, offset=4096)
+                else:
+                    h_bf[g, r0] = sb.tile([P, width, LANES], BF16, name="h_bf%d_%d" % (g, r0), align_bytes=64)
             nc.vector.tensor_tensor(
-                h_bf[g][:, r0:r1, :].rearrange("s (c q) j -> s c j q", q=LANES),
-                clipped[g][:, :, r0:r1].rearrange("s j (c q) -> s c j q", q=LANES),
-                wt_all[:, r0:r1].rearrange("s (c q) -> s c q", q=LANES).unsqueeze(2).to_broadcast([P, quads, LANES, LANES]),
+                h_bf[g, first][:, r0 - first:r1 - first, :].rearrange("s (c q) j -> s c j q", q=2),
+                clipped[g][:, :, r0:r1].rearrange("s j (c q) -> s c j q", q=2),
+                wt_all[:, r0:r1].rearrange("s (c q) -> s c q", q=2).unsqueeze(2).to_broadcast([P, pairs, LANES, 2]),
                 ALU.mult)
 
-        def quantise_h(g, r0, r1):
-            nc.vector.quantize_mx(hq[g][0][:, r0:r1].bitcast(E5M2), hq[g][1][:, r0:r1],
-                                  h_bf[g][:, r0:r1, :].rearrange("s r j -> s (r j)"))
+        def quantise_h(g, r0, r1, codes_tag=None):
+            codes, scales = mx_tiles("h%d_%d" % (g, r0), r1 - r0, codes_tag)
+            nc.vector.quantize_mx(codes[:].bitcast(E5M2), scales[:], h_bf[g, r0][:].rearrange("s r j -> s (r j)"))
+            for first in range(r0, r1, P):
+                cols = slice(first - r0, first - r0 + P)
+                hq[g, first // P] = codes[:, cols], scales[:, cols]
 
         for g in range(GROUPS):
             clipped[g] = sb.tile([P, LANES, R], F32, name="clipped%d" % g)
-            h_bf[g] = sb.tile([P, R, LANES], BF16, name="h_bf%d" % g, align_bytes=64)
-            hq[g] = mx_tiles("h%d" % g, R)
 
         x_bf = sb.tile([P, LANES, P, LANES], BF16, name="x_bf", tag="k_f32_00", align_bytes=64)
         x_codes, x_scales = mx_tiles("x", R)
         turn_k(0, 0, 4)
         turn_k(1, 0, 5)
-        deal(nc.scalar.copy, x_bf[:, :, 0:P // 2, :], x_raw[0][:])
         round_k(0, 1, 0, PASS // 2)
         round_k(0, 1, PASS // 2, PASS)
         round_k(1, 1, 0, PASS)
-        deal(nc.vector.tensor_copy, x_bf[:, :, P // 2:P, :], x_raw[1][:])
+        for a in range(2):
+            deal(nc.vector.tensor_copy, x_bf[:, :, a * (P // 2):(a + 1) * (P // 2), :], x_raw[a][:])
         quantise_k_along_d(0)
-        deal_y(0, LANES - 1, True)
         nc.vector.quantize_mx(x_codes[:].bitcast(E4M3), x_scales[:], x_bf[:].rearrange("p i m t -> p (i m t)"))
         quantise_k_along_d(1)
         for i in range(LANES):
@@ -222,12 +230,13 @@ def tile_attend_gpq_pl_hub_x_kernel(tc, xT, cb, norm, ts, y, wt, offs, out_0, ou
         weave_k(0, 0)
         weave_k(1, 0)
         diffs = {}
-        deal_y(1, LANES - 1, False)
         for j in range(LANES):
             score(0, j)
             diffs[0, j] = residual(0, j)
         for j in range(LANES):
             clip(0, j, diffs[0, j])
+        deal_y(1, 2)
+        deal_y(1, 3)
         for j in range(LANES):
             score(1, j)
         turn_k(0, 1, 2)
@@ -242,37 +251,38 @@ def tile_attend_gpq_pl_hub_x_kernel(tc, xT, cb, norm, ts, y, wt, offs, out_0, ou
         weigh(0, R // 2, R)
         quantise_h(0, 0, R // 2)
         quantise_k_along_n(0)
-        quantise_h(0, R // 2, R)
         for j in range(LANES):
             diffs[1, j] = residual(1, j)
         for j in range(LANES):
             clip(1, j, diffs[1, j])
+        quantise_h(0, R // 2, R, "ts_y6")
 
         grad = [sb.tile([P, 2, D], F32, name="grad%d" % u) for u in range(2)]
-        grad_bf = sb.tile([P, D, LANES], BF16, name="grad_bf", align_bytes=64)
         out_rows = out_0.rearrange("(p i) d -> p i d", i=LANES)
         acc = {}
         half = D // 2
 
         def second_pass(i, g):
-            cols = slice(i * P, (i + 1) * P)
-            nc.tensor.matmul_mx(acc[i][:], hq[g][0][:, cols].bitcast(E5M2), hq[g][1][:, cols],
+            nc.tensor.matmul_mx(acc[i][:], hq[g, i][0].bitcast(E5M2), hq[g, i][1],
                                 kn[g][0][:].bitcast(E4M3), kn[g][1][:], start=(g == 0), stop=(g == GROUPS - 1))
 
         def round_grad(engine_copy, u, cols):
             engine_copy(
-                grad_bf[:, cols, 2 * u:2 * u + 2].rearrange("p (c q) i -> p c i q", q=LANES),
-                grad[u][:, :, cols].rearrange("p i (c q) -> p c i q", q=LANES))
+                grad_bf[:, cols, 2 * u:2 * u + 2].rearrange("p (c q) i -> p c i q", q=2),
+                grad[u][:, :, cols].rearrange("p i (c q) -> p c i q", q=2))
 
         for i in range(LANES):
-            acc[i] = bank((3, 6, 0, 1)[i], [P, D])
+            acc[i] = bank((0, 1, 3, 6)[i], [P, D])
             second_pass(i, 0)
         weigh(1, 0, P)
+        quantise_k_along_n(1)
         for i in range(LANES):
-            if i + 1 < LANES:
-                weigh(1, (i + 1) * P, (i + 2) * P)
-            if i == 0:
-                quantise_k_along_n(1)
+            if i == 1:
+                weigh(1, P, 2 * P)
+            if i > 1:
+                weigh(1, i * P + P // 2, (i + 1) * P, i * P)
+            if 0 < i < LANES - 1:
+                weigh(1, (i + 1) * P, (i + 1) * P + P // 2)
             quantise_h(1, i * P, (i + 1) * P)
             second_pass(i, 1)
             for hh in range(2 if i == LANES - 1 else 1):
@@ -280,6 +290,7 @@ def tile_attend_gpq_pl_hub_x_kernel(tc, xT, cb, norm, ts, y, wt, offs, out_0, ou
                 nc.scalar.copy(grad[i // 2][:, i % 2, cols], acc[i][:, cols])
             nc.sync.dma_start(out_rows[:, i, :], grad[i // 2][:, i % 2, :])
 
+        grad_bf = sb.tile([P, D, LANES], BF16, name="grad_bf", tag="h_bf1_%d" % (R - P), align_bytes=64)
         g_codes, g_scales = mx_tiles("grad", D)
         words_out = out_1.rearrange("o p d b -> (o p) (d b)").bitcast(I32)
         round_grad(nc.vector.tensor_copy, 0, slice(0, D))

@@ -86,6 +86,9 @@ def tile_attend_gpq_pl_hub_x_kernel(tc, xT, cb, norm, ts, y, wt, offs, out_0, ou
         for i in range(LANES):
             nc.tensor.transpose(wt_all[:, i * P:(i + 1) * P], wt_col[:, i:i + 1].to_broadcast([P, P]), ident[:])
 
+        wt_last = sb.tile([P, P], F32, name="wt_last")
+        nc.scalar.copy(wt_last[:], wt_all[:, R - P:R])
+
         k_f32 = {}
         for g in range(GROUPS):
             for u in range(2):
@@ -139,7 +142,7 @@ def tile_attend_gpq_pl_hub_x_kernel(tc, xT, cb, norm, ts, y, wt, offs, out_0, ou
                 k_turned[g, u][:].rearrange("s j p -> s (j p)").bitcast(BF16).rearrange("s (j p e) -> s p e j", j=LANES, e=2))
 
         def quantise_k_along_n(g):
-            kn[g] = mx_tiles("kn%d" % g, D, ("diff3", "ts_y7")[g])
+            kn[g] = mx_tiles("kn%d" % g, D, ("diff2", "ts_y7")[g])
             nc.vector.quantize_mx(kn[g][0][:].bitcast(E4M3), kn[g][1][:], kn_bf[g][:].rearrange("s p u e j -> s (p u e j)"))
 
         def turn_y(g, j, i):
@@ -149,10 +152,9 @@ def tile_attend_gpq_pl_hub_x_kernel(tc, xT, cb, norm, ts, y, wt, offs, out_0, ou
             nc.tensor.transpose(y_turned[g, j][:, i * P:(i + 1) * P], cols, ident[:])
 
         def deal_y(g, i):
-            y_dealt[g, i] = laid.tile([P, LANES, P], F32, name="y_dealt%d" % i, align_bytes=64, offset=8192 + 2048 * (i - 2))
-            nc.gpsimd.tensor_scalar(y_dealt[g, i][:].rearrange("p j (c q) -> p c j q", q=LANES),
-                                    y_raw[g, i][:].rearrange("p (c q j) -> p c j q", q=LANES, j=LANES),
-                                    1.0, 0.0, ALU.mult, ALU.add)
+            y_dealt[g, i] = sb.tile([P, LANES, P], F32, name="y_dealt%d" % i, tag="diff0", align_bytes=64)
+            nc.scalar.copy(y_dealt[g, i][:].rearrange("p j (c q) -> p c j q", q=LANES),
+                           y_raw[g, i][:].rearrange("p (c q j) -> p c j q", q=LANES, j=LANES))
 
         def scale_y(g, j):
             col = g * LANES + j
@@ -170,8 +172,6 @@ def tile_attend_gpq_pl_hub_x_kernel(tc, xT, cb, norm, ts, y, wt, offs, out_0, ou
             col = g * LANES + j
             if g == 1:
                 diff = clipped[0][:, j, :]
-            elif j == 2:
-                diff = laid.tile([P, R], F32, name="diff2", align_bytes=64, offset=8192 + 1024)[:]
             else:
                 diff = sb.tile([P, R], F32, name="diff%d" % col, align_bytes=64)[:]
             nc.vector.scalar_tensor_tensor(diff, scores[g, j][:], ts_sq[:, col:col + 1], ts_y[g, j], ALU.mult, ALU.subtract)
@@ -194,10 +194,12 @@ def tile_attend_gpq_pl_hub_x_kernel(tc, xT, cb, norm, ts, y, wt, offs, out_0, ou
                     h_bf[g, r0] = laid.tile([P, width, LANES], BF16, name="h_bf_laid", align_bytes=64, offset=4096)
                 else:
                     h_bf[g, r0] = sb.tile([P, width, LANES], BF16, name="h_bf%d_%d" % (g, r0), align_bytes=64)
-            nc.vector.tensor_tensor(
+            on_gpsimd = (g, r0) == (0, R - P)
+            factors = wt_last[:] if on_gpsimd else wt_all[:, r0:r1]
+            (nc.gpsimd if on_gpsimd else nc.vector).tensor_tensor(
                 h_bf[g, first][:, r0 - first:r1 - first, :].rearrange("s (c q) j -> s c j q", q=2),
                 clipped[g][:, :, r0:r1].rearrange("s j (c q) -> s c j q", q=2),
-                wt_all[:, r0:r1].rearrange("s (c q) -> s c q", q=2).unsqueeze(2).to_broadcast([P, pairs, LANES, 2]),
+                factors.rearrange("s (c q) -> s c q", q=2).unsqueeze(2).to_broadcast([P, pairs, LANES, 2]),
                 ALU.mult)
 
         def quantise_h(g, r0, r1, codes_tag=None):
@@ -227,16 +229,15 @@ def tile_attend_gpq_pl_hub_x_kernel(tc, xT, cb, norm, ts, y, wt, offs, out_0, ou
                 turn_y(0, j, i)
         for j in range(LANES):
             scale_y(0, j)
-        weave_k(0, 0)
-        weave_k(1, 0)
         diffs = {}
         for j in range(LANES):
             score(0, j)
             diffs[0, j] = residual(0, j)
         for j in range(LANES):
             clip(0, j, diffs[0, j])
-        deal_y(1, 2)
+        weave_k(0, 0)
         deal_y(1, 3)
+        weave_k(1, 0)
         for j in range(LANES):
             score(1, j)
         turn_k(0, 1, 2)
@@ -248,14 +249,15 @@ def tile_attend_gpq_pl_hub_x_kernel(tc, xT, cb, norm, ts, y, wt, offs, out_0, ou
         turn_k(1, 1, 5)
         weave_k(1, 1)
         weigh(0, 0, R // 2)
-        weigh(0, R // 2, R)
+        weigh(0, R // 2, R - P)
+        weigh(0, R - P, R, R // 2)
         quantise_h(0, 0, R // 2)
         quantise_k_along_n(0)
+        quantise_h(0, R // 2, R)
         for j in range(LANES):
             diffs[1, j] = residual(1, j)
         for j in range(LANES):
             clip(1, j, diffs[1, j])
-        quantise_h(0, R // 2, R, "ts_y6")
 
         grad = [sb.tile([P, 2, D], F32, name="grad%d" % u) for u in range(2)]
         out_rows = out_0.rearrange("(p i) d -> p i d", i=LANES)
@@ -272,7 +274,7 @@ def tile_attend_gpq_pl_hub_x_kernel(tc, xT, cb, norm, ts, y, wt, offs, out_0, ou
                 grad[u][:, :, cols].rearrange("p i (c q) -> p c i q", q=2))
 
         for i in range(LANES):
-            acc[i] = bank((0, 1, 3, 6)[i], [P, D])
+            acc[i] = bank((3, 6, 0, 1)[i], [P, D])
             second_pass(i, 0)
         weigh(1, 0, P)
         quantise_k_along_n(1)

@@ -59,12 +59,13 @@ def tile_attend_gpq_pl_hub_x_kernel(tc, xT, cb, norm, ts, y, wt, offs, out_0, ou
                 y_raw[g, i] = sb.tile([P, PASS], F32, name="y_raw%d%d" % (g, i), align_bytes=64)
             nc.sync.dma_start(y_raw[g, i][:], y_rows[:, i, g * PASS:(g + 1) * PASS])
 
+        ts_col = sb.tile([P, GROUPS, LANES], F32, name="ts_col")
+        wt_col = sb.tile([P, LANES], F32, name="wt_col")
         for t in range(LANES):
             nc.sync.dma_start(book[t][:], cb_planes[:, t, :])
-        ts_col = sb.tile([P, GROUPS, LANES], F32, name="ts_col")
-        nc.scalar.dma_start(ts_col[:], ts[0:1, :].rearrange("o (g s j) -> (o s) g j", g=GROUPS, j=LANES))
-        wt_col = sb.tile([P, LANES], F32, name="wt_col")
-        nc.scalar.dma_start(wt_col[:], wt.rearrange("(p i) o -> p (i o)", i=LANES))
+            if t == 0:
+                nc.sync.dma_start(ts_col[:], ts[0:1, :].rearrange("o (g s j) -> (o s) g j", g=GROUPS, j=LANES))
+                nc.sync.dma_start(wt_col[:], wt.rearrange("(p i) o -> p (i o)", i=LANES))
         for g in range(GROUPS):
             for i in range(LANES):
                 load_y(g, i)
@@ -80,7 +81,9 @@ def tile_attend_gpq_pl_hub_x_kernel(tc, xT, cb, norm, ts, y, wt, offs, out_0, ou
             spread = bank(4 + g, [P, LANES, P])
             for c in range(LANES):
                 nc.tensor.transpose(spread[:, c, :], norm_col[:, g, c:c + 1].to_broadcast([P, P]), ident[:])
-            (nc.scalar.copy, nc.vector.tensor_copy)[g](norm_all[g][:].rearrange("p (m c) -> p m c", c=LANES), spread[:].rearrange("p c m -> p m c"))
+            (nc.vector.tensor_copy, nc.scalar.copy)[g](norm_all[g][:].rearrange("p (m c) -> p m c", c=LANES), spread[:].rearrange("p c m -> p m c"))
+        norm_later = sb.tile([P, PASS], F32, name="norm_later")
+        nc.scalar.copy(norm_later[:], norm_all[0][:])
 
         wt_all = bank(7, [P, R])
         for i in range(LANES):
@@ -92,7 +95,10 @@ def tile_attend_gpq_pl_hub_x_kernel(tc, xT, cb, norm, ts, y, wt, offs, out_0, ou
         k_f32 = {}
         for g in range(GROUPS):
             for u in range(2):
-                k_f32[g, u] = sb.tile([P, 2, PASS], F32, name="k_f32_%d%d" % (g, u), align_bytes=64)
+                if (g, u) == (0, 0):
+                    k_f32[g, u] = laid.tile([P, 2, PASS], F32, name="k_f32_00", align_bytes=64, offset=8192)
+                else:
+                    k_f32[g, u] = sb.tile([P, 2, PASS], F32, name="k_f32_%d%d" % (g, u), align_bytes=64)
         k_bf = [sb.tile([P, LANES, P, LANES], BF16, name="k_bf%d" % g, align_bytes=64) for g in range(GROUPS)]
 
         def round_k(g, u, n0, n1):
@@ -102,7 +108,7 @@ def tile_attend_gpq_pl_hub_x_kernel(tc, xT, cb, norm, ts, y, wt, offs, out_0, ou
             first = g * PASS
             nc.vector.tensor_tensor(
                 k_f32[g, t // 2][:, t % 2, n0:n1], book[t][:].indirect(lists[:, (first + n0) // 16:(first + n1) // 16]),
-                norm_all[g][:, n0:n1], ALU.mult)
+                (norm_later if g == 0 and t > 0 else norm_all[g])[:, n0:n1], ALU.mult)
 
         for t in range(LANES):
             for g in range(GROUPS):
@@ -125,7 +131,11 @@ def tile_attend_gpq_pl_hub_x_kernel(tc, xT, cb, norm, ts, y, wt, offs, out_0, ou
         kd, kn, kn_bf, clipped, h_bf, hq, y_turned, ts_y, scores, k_turned, y_dealt = {}, {}, {}, {}, {}, {}, {}, {}, {}, {}, {}
 
         def quantise_k_along_d(g):
-            kd[g] = mx_tiles("kd%d" % g, PASS, ("x_raw1", "k_f32_00")[g])
+            if g == 0:
+                kd[g] = mx_tiles("kd0", PASS, "x_raw1")
+            else:
+                kd[g] = (laid.tile([P, PASS], U32, name="kd1_codes", align_bytes=64, offset=8192),
+                         sb.tile([P, PASS], U8, name="kd1_scales", align_bytes=64))
             nc.vector.quantize_mx(kd[g][0][:].bitcast(E4M3), kd[g][1][:], k_bf[g][:].rearrange("p j s t -> p (j s t)"))
 
         def turn_k(g, u, b):
@@ -147,14 +157,14 @@ def tile_attend_gpq_pl_hub_x_kernel(tc, xT, cb, norm, ts, y, wt, offs, out_0, ou
 
         def turn_y(g, j, i):
             if i == 0:
-                y_turned[g, j] = bank((0, 1, 2, 3, 4, 5, 2, 4)[g * LANES + j], [P, R])
+                y_turned[g, j] = bank((0, 1, 2, 3, 2, 5, 4, 2)[g * LANES + j], [P, R])
             cols = y_dealt[g, i][:, j, :] if (g, i) in y_dealt else y_raw[g, i][:, j:PASS:LANES]
             nc.tensor.transpose(y_turned[g, j][:, i * P:(i + 1) * P], cols, ident[:])
 
         def deal_y(g, i):
-            y_dealt[g, i] = sb.tile([P, LANES, P], F32, name="y_dealt%d" % i, tag="diff0", align_bytes=64)
-            nc.scalar.copy(y_dealt[g, i][:].rearrange("p j (c q) -> p c j q", q=LANES),
-                           y_raw[g, i][:].rearrange("p (c q j) -> p c j q", q=LANES, j=LANES))
+            y_dealt[g, i] = laid.tile([P, LANES, P], F32, name="y_dealt%d" % i, align_bytes=64, offset=10240)
+            nc.gpsimd.tensor_scalar(y_dealt[g, i][:].rearrange("p j (c q) -> p c j q", q=LANES),
+                                    y_raw[g, i][:].rearrange("p (c q j) -> p c j q", q=LANES, j=LANES), 1.0, 0.0, ALU.mult, ALU.add)
 
         def scale_y(g, j):
             col = g * LANES + j
@@ -212,7 +222,7 @@ def tile_attend_gpq_pl_hub_x_kernel(tc, xT, cb, norm, ts, y, wt, offs, out_0, ou
         for g in range(GROUPS):
             clipped[g] = sb.tile([P, LANES, R], F32, name="clipped%d" % g)
 
-        x_bf = sb.tile([P, LANES, P, LANES], BF16, name="x_bf", tag="k_f32_00", align_bytes=64)
+        x_bf = laid.tile([P, LANES, P, LANES], BF16, name="x_bf", align_bytes=64, offset=8192)
         x_codes, x_scales = mx_tiles("x", R)
         turn_k(0, 0, 4)
         turn_k(1, 0, 5)
@@ -224,6 +234,7 @@ def tile_attend_gpq_pl_hub_x_kernel(tc, xT, cb, norm, ts, y, wt, offs, out_0, ou
         quantise_k_along_d(0)
         nc.vector.quantize_mx(x_codes[:].bitcast(E4M3), x_scales[:], x_bf[:].rearrange("p i m t -> p (i m t)"))
         quantise_k_along_d(1)
+        deal_y(1, 0)
         for i in range(LANES):
             for j in range(LANES):
                 turn_y(0, j, i)
@@ -236,11 +247,10 @@ def tile_attend_gpq_pl_hub_x_kernel(tc, xT, cb, norm, ts, y, wt, offs, out_0, ou
         for j in range(LANES):
             clip(0, j, diffs[0, j])
         weave_k(0, 0)
-        deal_y(1, 3)
         weave_k(1, 0)
         for j in range(LANES):
             score(1, j)
-        turn_k(0, 1, 2)
+        turn_k(0, 1, 4)
         weave_k(0, 1)
         for j in range(LANES):
             for i in range(LANES):
@@ -274,7 +284,7 @@ def tile_attend_gpq_pl_hub_x_kernel(tc, xT, cb, norm, ts, y, wt, offs, out_0, ou
                 grad[u][:, :, cols].rearrange("p i (c q) -> p c i q", q=2))
 
         for i in range(LANES):
-            acc[i] = bank((3, 6, 0, 1)[i], [P, D])
+            acc[i] = bank((6, 0, 1, 5)[i], [P, D])
             second_pass(i, 0)
         weigh(1, 0, P)
         quantise_k_along_n(1)

@@ -157,7 +157,7 @@ def tile_attend_gpq_pl_hub_x_kernel(tc, xT, cb, norm, ts, y, wt, offs, out_0, ou
 
         def turn_y(g, j, i):
             if i == 0:
-                y_turned[g, j] = bank((0, 1, 2, 3, 2, 5, 4, 2)[g * LANES + j], [P, R])
+                y_turned[g, j] = bank((0, 1, 2, 3, 2, 4, 5, 2)[g * LANES + j], [P, R])
             cols = y_dealt[g, i][:, j, :] if (g, i) in y_dealt else y_raw[g, i][:, j:PASS:LANES]
             nc.tensor.transpose(y_turned[g, j][:, i * P:(i + 1) * P], cols, ident[:])
 
@@ -200,7 +200,7 @@ def tile_attend_gpq_pl_hub_x_kernel(tc, xT, cb, norm, ts, y, wt, offs, out_0, ou
             first = r0 if tile_first is None else tile_first
             width = R // 2 if g == 0 else P
             if first == r0:
-                if (g, r0) == (1, P):
+                if (g, r0) == (1, 2 * P):
                     h_bf[g, r0] = laid.tile([P, width, LANES], BF16, name="h_bf_laid", align_bytes=64, offset=4096)
                 else:
                     h_bf[g, r0] = sb.tile([P, width, LANES], BF16, name="h_bf%d_%d" % (g, r0), align_bytes=64)
@@ -225,10 +225,10 @@ def tile_attend_gpq_pl_hub_x_kernel(tc, xT, cb, norm, ts, y, wt, offs, out_0, ou
         x_bf = laid.tile([P, LANES, P, LANES], BF16, name="x_bf", align_bytes=64, offset=8192)
         x_codes, x_scales = mx_tiles("x", R)
         turn_k(0, 0, 4)
-        turn_k(1, 0, 5)
         round_k(0, 1, 0, PASS // 2)
         round_k(0, 1, PASS // 2, PASS)
         round_k(1, 1, 0, PASS)
+        turn_k(0, 1, 5)
         for a in range(2):
             deal(nc.vector.tensor_copy, x_bf[:, :, a * (P // 2):(a + 1) * (P // 2), :], x_raw[a][:])
         quantise_k_along_d(0)
@@ -247,17 +247,16 @@ def tile_attend_gpq_pl_hub_x_kernel(tc, xT, cb, norm, ts, y, wt, offs, out_0, ou
         for j in range(LANES):
             clip(0, j, diffs[0, j])
         weave_k(0, 0)
-        weave_k(1, 0)
+        weave_k(0, 1)
         for j in range(LANES):
             score(1, j)
-        turn_k(0, 1, 4)
-        weave_k(0, 1)
         for j in range(LANES):
             for i in range(LANES):
                 turn_y(1, j, i)
             scale_y(1, j)
-        turn_k(1, 1, 5)
-        weave_k(1, 1)
+        for u in range(2):
+            turn_k(1, u, 4 + u)
+            weave_k(1, u)
         weigh(0, 0, R // 2)
         weigh(0, R // 2, R - P)
         weigh(0, R - P, R, R // 2)
@@ -284,13 +283,12 @@ def tile_attend_gpq_pl_hub_x_kernel(tc, xT, cb, norm, ts, y, wt, offs, out_0, ou
                 grad[u][:, :, cols].rearrange("p i (c q) -> p c i q", q=2))
 
         for i in range(LANES):
-            acc[i] = bank((6, 0, 1, 5)[i], [P, D])
+            acc[i] = bank((6, 0, 1, 2)[i], [P, D])
             second_pass(i, 0)
         weigh(1, 0, P)
+        weigh(1, P, 2 * P)
         quantise_k_along_n(1)
         for i in range(LANES):
-            if i == 1:
-                weigh(1, P, 2 * P)
             if i > 1:
                 weigh(1, i * P + P // 2, (i + 1) * P, i * P)
             if 0 < i < LANES - 1:

@@ -41,14 +41,15 @@ def tile_attend_gpq_pl_hub_x_kernel(tc, xT, cb, norm, ts, y, wt, offs, out_0, ou
         def deal(engine_copy, dst, src):
             engine_copy(dst.rearrange("p j s t -> p s t j"), src.rearrange("p t (s j) -> p s t j", j=LANES))
 
-        lists = sb.tile([P, N // 16], U16, name="lists")
-        nc.sync.dma_start(lists[:], offs)
         norm_col = sb.tile([P, GROUPS, LANES], F32, name="norm_col")
         nc.sync.dma_start(norm_col[:], norm[0:1, :].rearrange("o (g m c) -> (o m) g c", g=GROUPS, c=LANES))
+        lists = sb.tile([P, N // 16], U16, name="lists")
+        nc.sync.dma_start(lists[:], offs)
         cb_planes = cb.rearrange("(p t) c -> p t c", t=LANES)
         book = [sb.tile([P, C], F32, name="book%d" % t) for t in range(LANES)]
         x_planes = xT.rearrange("(p t) r -> p t r", t=LANES)
-        x_raw = [sb.tile([P, LANES, R // 2], F32, name="x_raw%d" % a, align_bytes=64) for a in range(2)]
+        x_raw = [sb.tile([P, LANES, R // 2], F32, name="x_raw0", align_bytes=64),
+                 laid.tile([P, LANES, R // 2], F32, name="x_raw1", align_bytes=64, offset=12288)]
         y_rows = y.rearrange("(p i) n -> p i n", i=LANES)
         y_raw = {}
 
@@ -89,8 +90,9 @@ def tile_attend_gpq_pl_hub_x_kernel(tc, xT, cb, norm, ts, y, wt, offs, out_0, ou
         for i in range(LANES):
             nc.tensor.transpose(wt_all[:, i * P:(i + 1) * P], wt_col[:, i:i + 1].to_broadcast([P, P]), ident[:])
 
-        wt_last = sb.tile([P, P], F32, name="wt_last")
-        nc.scalar.copy(wt_last[:], wt_all[:, R - P:R])
+        shared = R - 3 * P // 4
+        wt_last = sb.tile([P, R - shared], F32, name="wt_last")
+        nc.scalar.copy(wt_last[:], wt_all[:, shared:R])
 
         k_f32 = {}
         for g in range(GROUPS):
@@ -131,11 +133,8 @@ def tile_attend_gpq_pl_hub_x_kernel(tc, xT, cb, norm, ts, y, wt, offs, out_0, ou
         kd, kn, kn_bf, clipped, h_bf, hq, y_turned, ts_y, scores, k_turned, y_dealt = {}, {}, {}, {}, {}, {}, {}, {}, {}, {}, {}
 
         def quantise_k_along_d(g):
-            if g == 0:
-                kd[g] = mx_tiles("kd0", PASS, "x_raw1")
-            else:
-                kd[g] = (laid.tile([P, PASS], U32, name="kd1_codes", align_bytes=64, offset=8192),
-                         sb.tile([P, PASS], U8, name="kd1_scales", align_bytes=64))
+            kd[g] = (laid.tile([P, PASS], U32, name="kd%d_codes" % g, align_bytes=64, offset=12288 + 2048 * g),
+                     sb.tile([P, PASS], U8, name="kd%d_scales" % g, align_bytes=64))
             nc.vector.quantize_mx(kd[g][0][:].bitcast(E4M3), kd[g][1][:], k_bf[g][:].rearrange("p j s t -> p (j s t)"))
 
         def turn_k(g, u, b):
@@ -180,10 +179,8 @@ def tile_attend_gpq_pl_hub_x_kernel(tc, xT, cb, norm, ts, y, wt, offs, out_0, ou
 
         def residual(g, j):
             col = g * LANES + j
-            if g == 1:
-                diff = clipped[0][:, j, :]
-            else:
-                diff = sb.tile([P, R], F32, name="diff%d" % col, align_bytes=64)[:]
+            tag = "diff%d" % col
+            diff = sb.tile([P, R], F32, name="diff%d" % col, tag=tag, align_bytes=64)[:]
             nc.vector.scalar_tensor_tensor(diff, scores[g, j][:], ts_sq[:, col:col + 1], ts_y[g, j], ALU.mult, ALU.subtract)
             return diff
 
@@ -198,19 +195,35 @@ def tile_attend_gpq_pl_hub_x_kernel(tc, xT, cb, norm, ts, y, wt, offs, out_0, ou
         def weigh(g, r0, r1, tile_first=None):
             pairs = (r1 - r0) // 2
             first = r0 if tile_first is None else tile_first
-            width = R // 2 if g == 0 else P
+            width = R // 2 if (g, r0) == (0, 0) else P
             if first == r0:
                 if (g, r0) == (1, 2 * P):
                     h_bf[g, r0] = laid.tile([P, width, LANES], BF16, name="h_bf_laid", align_bytes=64, offset=4096)
                 else:
                     h_bf[g, r0] = sb.tile([P, width, LANES], BF16, name="h_bf%d_%d" % (g, r0), align_bytes=64)
-            on_gpsimd = (g, r0) == (0, R - P)
+            on_gpsimd = (g, r0) == (0, shared)
             factors = wt_last[:] if on_gpsimd else wt_all[:, r0:r1]
             (nc.gpsimd if on_gpsimd else nc.vector).tensor_tensor(
                 h_bf[g, first][:, r0 - first:r1 - first, :].rearrange("s (c q) j -> s c j q", q=2),
                 clipped[g][:, :, r0:r1].rearrange("s j (c q) -> s c j q", q=2),
                 factors.rearrange("s (c q) -> s c q", q=2).unsqueeze(2).to_broadcast([P, pairs, LANES, 2]),
                 ALU.mult)
+
+        def weigh_turned(g, i, b, b_back, first):
+            turned = bank(b, [P, LANES, P])
+            for j in range(LANES):
+                nc.tensor.transpose(turned[:, j, :], clipped[g][:, j, i * P:(i + 1) * P], ident[:])
+            by_row = sb.tile([P, 2, P, 2], BF16, name="by_row%d" % g, align_bytes=64)
+            nc.scalar.activation(by_row[:], turned[:].rearrange("m (v e) s -> m v s e", e=2), ACT.Copy, scale=wt_col[:, i:i + 1])
+            words = by_row[:].rearrange("m v s e -> m (v s e)").bitcast(F32)
+
+            def turn_back():
+                back = bank(b_back, [P, 2, P])
+                for v in range(2):
+                    nc.tensor.transpose(back[:, v, :], words[:, v * P:(v + 1) * P], ident[:])
+                rows = h_bf[g, first][:, i * P - first:(i + 1) * P - first, :].rearrange("s m j -> s (m j)").bitcast(F32)
+                nc.scalar.copy(rows.rearrange("s (m v) -> s m v", v=2), back[:].rearrange("s v m -> s m v"))
+            return turn_back
 
         def quantise_h(g, r0, r1, codes_tag=None):
             codes, scales = mx_tiles("h%d_%d" % (g, r0), r1 - r0, codes_tag)
@@ -258,15 +271,17 @@ def tile_attend_gpq_pl_hub_x_kernel(tc, xT, cb, norm, ts, y, wt, offs, out_0, ou
             turn_k(1, u, 4 + u)
             weave_k(1, u)
         weigh(0, 0, R // 2)
-        weigh(0, R // 2, R - P)
-        weigh(0, R - P, R, R // 2)
+        h_bf[0, R // 2] = sb.tile([P, P, LANES], BF16, name="h_bf0_256", align_bytes=64)
+        weigh(0, R - P, shared)
+        weigh(0, shared, R, R - P)
         quantise_h(0, 0, R // 2)
         quantise_k_along_n(0)
-        quantise_h(0, R // 2, R)
+        quantise_h(0, R - P, R)
         for j in range(LANES):
             diffs[1, j] = residual(1, j)
         for j in range(LANES):
             clip(1, j, diffs[1, j])
+        weigh_turned(0, 2, 4, 5, R // 2)()
 
         grad = [sb.tile([P, 2, D], F32, name="grad%d" % u) for u in range(2)]
         out_rows = out_0.rearrange("(p i) d -> p i d", i=LANES)
@@ -282,13 +297,20 @@ def tile_attend_gpq_pl_hub_x_kernel(tc, xT, cb, norm, ts, y, wt, offs, out_0, ou
                 grad_bf[:, cols, 2 * u:2 * u + 2].rearrange("p (c q) i -> p c i q", q=2),
                 grad[u][:, :, cols].rearrange("p i (c q) -> p c i q", q=2))
 
-        for i in range(LANES):
-            acc[i] = bank((6, 0, 1, 2)[i], [P, D])
+        def open_sum(i):
+            acc[i] = bank((0, 4, 6, 1)[i], [P, D])
             second_pass(i, 0)
+
+        open_sum(0)
+        open_sum(3)
+        open_sum(1)
         weigh(1, 0, P)
         weigh(1, P, 2 * P)
         quantise_k_along_n(1)
         for i in range(LANES):
+            if i == 2:
+                quantise_h(0, R // 2, R - P)
+                open_sum(2)
             if i > 1:
                 weigh(1, i * P + P // 2, (i + 1) * P, i * P)
             if 0 < i < LANES - 1:

@@ -77,7 +77,7 @@ def tile_attend_gpq_pl_hub_x_kernel(tc, xT, cb, norm, ts, y, wt, offs, out_0, ou
         ident = sb.tile([P, P], F32, name="ident")
         make_identity(nc, ident[:])
 
-        norm_all = [sb.tile([P, PASS], F32, name="norm_all%d" % g) for g in range(GROUPS)]
+        norm_all = [laid.tile([P, PASS], F32, name="norm_all0", align_bytes=64, offset=23552), sb.tile([P, PASS], F32, name="norm_all1")]
         for g in range(GROUPS):
             spread = bank(4 + g, [P, LANES, P])
             for c in range(LANES):
@@ -99,6 +99,8 @@ def tile_attend_gpq_pl_hub_x_kernel(tc, xT, cb, norm, ts, y, wt, offs, out_0, ou
             for u in range(2):
                 if (g, u) == (0, 0):
                     k_f32[g, u] = laid.tile([P, 2, PASS], F32, name="k_f32_00", align_bytes=64, offset=8192)
+                elif u == 1:
+                    k_f32[g, u] = laid.tile([P, 2, PASS], F32, name="k_f32_%d1" % g, align_bytes=64, offset=20480 + 4096 * g)
                 else:
                     k_f32[g, u] = sb.tile([P, 2, PASS], F32, name="k_f32_%d%d" % (g, u), align_bytes=64)
         k_bf = [sb.tile([P, LANES, P, LANES], BF16, name="k_bf%d" % g, align_bytes=64) for g in range(GROUPS)]
@@ -113,8 +115,13 @@ def tile_attend_gpq_pl_hub_x_kernel(tc, xT, cb, norm, ts, y, wt, offs, out_0, ou
                 (norm_later if g == 0 and t > 0 else norm_all[g])[:, n0:n1], ALU.mult)
 
         for t in range(LANES):
+            if t == 1:
+                picked = laid.tile([P, PASS], F32, name="picked", align_bytes=64, offset=23552)
+                nc.scalar.activation(picked[:], book[t][:].indirect(lists[:, PASS // 16:N // 16]), ACT.Copy)
             for g in range(GROUPS):
-                if (t, g) == (LANES - 1, 0):
+                if (t, g) == (1, 1):
+                    nc.vector.tensor_tensor(k_f32[g, 0][:, t, :], picked[:], norm_all[g][:], ALU.mult)
+                elif (t, g) == (LANES - 1, 0):
                     gather(t, g, 0, PASS // 2)
                     gather(t, g, PASS // 2, PASS)
                 else:

@@ -91,8 +91,9 @@ def tile_attend_gpq_pl_hub_x_kernel(tc, xT, cb, norm, ts, y, wt, offs, out_0, ou
             nc.tensor.transpose(wt_all[:, i * P:(i + 1) * P], wt_col[:, i:i + 1].to_broadcast([P, P]), ident[:])
 
         shared = R - 3 * P // 4
-        wt_last = sb.tile([P, R - shared], F32, name="wt_last")
-        nc.scalar.copy(wt_last[:], wt_all[:, shared:R])
+        shared_late = shared - P
+        wt_last = sb.tile([P, R - shared_late], F32, name="wt_last")
+        nc.scalar.copy(wt_last[:], wt_all[:, shared_late:R])
 
         k_f32 = {}
         for g in range(GROUPS):
@@ -204,16 +205,24 @@ def tile_attend_gpq_pl_hub_x_kernel(tc, xT, cb, norm, ts, y, wt, offs, out_0, ou
             first = r0 if tile_first is None else tile_first
             width = R // 2 if (g, r0) == (0, 0) else P
             if first == r0:
-                if (g, r0) == (1, 2 * P):
+                if (g, r0) == (1, 3 * P):
                     h_bf[g, r0] = laid.tile([P, width, LANES], BF16, name="h_bf_laid", align_bytes=64, offset=4096)
                 else:
                     h_bf[g, r0] = sb.tile([P, width, LANES], BF16, name="h_bf%d_%d" % (g, r0), align_bytes=64)
-            on_gpsimd = (g, r0) == (0, shared)
-            factors = wt_last[:] if on_gpsimd else wt_all[:, r0:r1]
+            on_gpsimd = (g, r0) in ((0, shared), (1, shared_late))
+            factors = wt_last[:, r0 - shared_late:r1 - shared_late] if on_gpsimd else wt_all[:, r0:r1]
             (nc.gpsimd if on_gpsimd else nc.vector).tensor_tensor(
                 h_bf[g, first][:, r0 - first:r1 - first, :].rearrange("s (c q) j -> s c j q", q=2),
                 clipped[g][:, :, r0:r1].rearrange("s j (c q) -> s c j q", q=2),
                 factors.rearrange("s (c q) -> s c q", q=2).unsqueeze(2).to_broadcast([P, pairs, LANES, 2]),
+                ALU.mult)
+
+        def weigh_part(r0, r1):
+            pairs = (r1 - r0) // 2
+            nc.vector.tensor_tensor(
+                h_bf[1, r0][:, 0:r1 - r0, :].rearrange("s (c q) j -> s c j q", q=2),
+                clipped[1][:, :, r0:r1].rearrange("s j (c q) -> s c j q", q=2),
+                wt_all[:, r0:r1].rearrange("s (c q) -> s c q", q=2).unsqueeze(2).to_broadcast([P, pairs, LANES, 2]),
                 ALU.mult)
 
         def weigh_turned(g, i, b, b_back, first):
@@ -296,8 +305,9 @@ def tile_attend_gpq_pl_hub_x_kernel(tc, xT, cb, norm, ts, y, wt, offs, out_0, ou
         half = D // 2
 
         def second_pass(i, g):
-            nc.tensor.matmul_mx(acc[i][:], hq[g, i][0].bitcast(E5M2), hq[g, i][1],
-                                kn[g][0][:].bitcast(E4M3), kn[g][1][:], start=(g == 0), stop=(g == GROUPS - 1))
+            for cols, part in acc[i]:
+                nc.tensor.matmul_mx(part[:], hq[g, i][0].bitcast(E5M2), hq[g, i][1],
+                                    kn[g][0][:, cols].bitcast(E4M3), kn[g][1][:, cols], start=(g == 0), stop=(g == GROUPS - 1))
 
         def round_grad(engine_copy, u, cols):
             engine_copy(
@@ -305,12 +315,17 @@ def tile_attend_gpq_pl_hub_x_kernel(tc, xT, cb, norm, ts, y, wt, offs, out_0, ou
                 grad[u][:, :, cols].rearrange("p i (c q) -> p c i q", q=2))
 
         def open_sum(i):
-            acc[i] = bank((0, 4, 6, 1)[i], [P, D])
+            if i == LANES - 1:
+                acc[i] = [(slice(hh * half, (hh + 1) * half), bank(1 + hh, [P, half])) for hh in range(2)]
+            else:
+                acc[i] = [(slice(0, D), bank((0, 4, 6)[i], [P, D]))]
             second_pass(i, 0)
 
         open_sum(0)
         open_sum(3)
         open_sum(1)
+        h_bf[1, 2 * P] = sb.tile([P, P, LANES], BF16, name="h_bf1_256", align_bytes=64)
+        weigh(1, shared_late, 3 * P, 2 * P)
         weigh(1, 0, P)
         weigh(1, P, 2 * P)
         quantise_k_along_n(1)
@@ -318,18 +333,19 @@ def tile_attend_gpq_pl_hub_x_kernel(tc, xT, cb, norm, ts, y, wt, offs, out_0, ou
             if i == 2:
                 quantise_h(0, R // 2, R - P)
                 open_sum(2)
-            if i > 1:
-                weigh(1, i * P + P // 2, (i + 1) * P, i * P)
-            if 0 < i < LANES - 1:
-                weigh(1, (i + 1) * P, (i + 1) * P + P // 2)
+            if i == 1:
+                weigh_part(2 * P, shared_late)
+            if i == 2:
+                weigh(1, 3 * P, 3 * P + P // 2)
+            if i == 3:
+                weigh(1, 3 * P + P // 2, R, 3 * P)
             quantise_h(1, i * P, (i + 1) * P)
             second_pass(i, 1)
-            for hh in range(2 if i == LANES - 1 else 1):
-                cols = slice(hh * half, (hh + 1) * half) if i == LANES - 1 else slice(0, D)
-                nc.scalar.copy(grad[i // 2][:, i % 2, cols], acc[i][:, cols])
+            for cols, part in acc[i]:
+                nc.scalar.copy(grad[i // 2][:, i % 2, cols], part[:])
             nc.sync.dma_start(out_rows[:, i, :], grad[i // 2][:, i % 2, :])
 
-        grad_bf = sb.tile([P, D, LANES], BF16, name="grad_bf", tag="h_bf1_%d" % (R - P), align_bytes=64)
+        grad_bf = laid.tile([P, D, LANES], BF16, name="grad_bf", align_bytes=64, offset=4096)
         g_codes, g_scales = mx_tiles("grad", D)
         words_out = out_1.rearrange("o p d b -> (o p) (d b)").bitcast(I32)
         round_grad(nc.vector.tensor_copy, 0, slice(0, D))

@@ -90,10 +90,8 @@ def tile_attend_gpq_pl_hub_x_kernel(tc, xT, cb, norm, ts, y, wt, offs, out_0, ou
         for i in range(LANES):
             nc.tensor.transpose(wt_all[:, i * P:(i + 1) * P], wt_col[:, i:i + 1].to_broadcast([P, P]), ident[:])
 
-        shared = R - 3 * P // 4
-        shared_late = shared - P
-        wt_last = sb.tile([P, R - shared_late], F32, name="wt_last")
-        nc.scalar.copy(wt_last[:], wt_all[:, shared_late:R])
+        wt_rows = sb.tile([P, R - P], F32, name="wt_rows")
+        nc.scalar.copy(wt_rows[:], wt_all[:, P:R])
 
         k_f32 = {}
         for g in range(GROUPS):
@@ -200,30 +198,20 @@ def tile_attend_gpq_pl_hub_x_kernel(tc, xT, cb, norm, ts, y, wt, offs, out_0, ou
                 engine.tensor_scalar(clipped[g][:, j, rows], diff[:, rows], ts_hi[:, col:col + 1], ts_lo[:, col:col + 1],
                                      ALU.min, ALU.max)
 
-        def weigh(g, r0, r1, tile_first=None):
-            pairs = (r1 - r0) // 2
-            first = r0 if tile_first is None else tile_first
-            width = R // 2 if (g, r0) == (0, 0) else P
-            if first == r0:
-                if (g, r0) == (1, 3 * P):
-                    h_bf[g, r0] = laid.tile([P, width, LANES], BF16, name="h_bf_laid", align_bytes=64, offset=4096)
-                else:
-                    h_bf[g, r0] = sb.tile([P, width, LANES], BF16, name="h_bf%d_%d" % (g, r0), align_bytes=64)
-            on_gpsimd = (g, r0) in ((0, shared), (1, shared_late))
-            factors = wt_last[:, r0 - shared_late:r1 - shared_late] if on_gpsimd else wt_all[:, r0:r1]
-            (nc.gpsimd if on_gpsimd else nc.vector).tensor_tensor(
-                h_bf[g, first][:, r0 - first:r1 - first, :].rearrange("s (c q) j -> s c j q", q=2),
+        def weigh(engine, g, i, m0, m1):
+            r0, r1 = i * P + m0, i * P + m1
+            factors = wt_rows[:, r0 - P:r1 - P] if engine is nc.gpsimd else wt_all[:, r0:r1]
+            engine.tensor_tensor(
+                h_bf[g, i * P][:, m0:m1, :].rearrange("s (c q) j -> s c j q", q=2),
                 clipped[g][:, :, r0:r1].rearrange("s j (c q) -> s c j q", q=2),
-                factors.rearrange("s (c q) -> s c q", q=2).unsqueeze(2).to_broadcast([P, pairs, LANES, 2]),
+                factors.rearrange("s (c q) -> s c q", q=2).unsqueeze(2).to_broadcast([P, (m1 - m0) // 2, LANES, 2]),
                 ALU.mult)
 
-        def weigh_part(r0, r1):
-            pairs = (r1 - r0) // 2
-            nc.vector.tensor_tensor(
-                h_bf[1, r0][:, 0:r1 - r0, :].rearrange("s (c q) j -> s c j q", q=2),
-                clipped[1][:, :, r0:r1].rearrange("s j (c q) -> s c j q", q=2),
-                wt_all[:, r0:r1].rearrange("s (c q) -> s c q", q=2).unsqueeze(2).to_broadcast([P, pairs, LANES, 2]),
-                ALU.mult)
+        def h_tile(g, i, offset=None):
+            if offset is None:
+                h_bf[g, i * P] = sb.tile([P, P, LANES], BF16, name="h_bf%d_%d" % (g, i), align_bytes=64)
+            else:
+                h_bf[g, i * P] = laid.tile([P, P, LANES], BF16, name="h_bf%d_%d" % (g, i), align_bytes=64, offset=offset)
 
         def weigh_turned(g, i, b, b_back, first):
             turned = bank(b, [P, LANES, P])
@@ -286,13 +274,17 @@ def tile_attend_gpq_pl_hub_x_kernel(tc, xT, cb, norm, ts, y, wt, offs, out_0, ou
         for u in range(2):
             turn_k(1, u, 4 + u)
             weave_k(1, u)
-        weigh(0, 0, R // 2)
-        h_bf[0, R // 2] = sb.tile([P, P, LANES], BF16, name="h_bf0_256", align_bytes=64)
-        weigh(0, R - P, shared)
-        weigh(0, shared, R, R - P)
-        quantise_h(0, 0, R // 2)
+        for i in (0, 2, 3):
+            h_tile(0, i)
+        weigh(nc.vector, 0, 0, 0, P)
+        weigh(nc.vector, 0, 3, 0, P // 2)
+        weigh(nc.gpsimd, 0, 3, P // 2, P)
+        quantise_h(0, 0, P)
         quantise_k_along_n(0)
         quantise_h(0, R - P, R)
+        h_tile(0, 1, 0)
+        weigh(nc.gpsimd, 0, 1, P // 4, P)
+        weigh(nc.vector, 0, 1, 0, P // 4)
         for j in range(LANES):
             diffs[1, j] = residual(1, j)
         for j in range(LANES):
@@ -323,22 +315,25 @@ def tile_attend_gpq_pl_hub_x_kernel(tc, xT, cb, norm, ts, y, wt, offs, out_0, ou
 
         open_sum(0)
         open_sum(3)
+        for i in range(3):
+            h_tile(1, i)
+        weigh(nc.gpsimd, 1, 2, P // 4, P)
+        weigh(nc.vector, 1, 0, 0, P)
+        weigh(nc.vector, 1, 1, 0, P)
+        quantise_h(0, P, 2 * P)
         open_sum(1)
-        h_bf[1, 2 * P] = sb.tile([P, P, LANES], BF16, name="h_bf1_256", align_bytes=64)
-        weigh(1, shared_late, 3 * P, 2 * P)
-        weigh(1, 0, P)
-        weigh(1, P, 2 * P)
         quantise_k_along_n(1)
+        h_tile(1, 3, 4096)
         for i in range(LANES):
             if i == 2:
                 quantise_h(0, R // 2, R - P)
                 open_sum(2)
             if i == 1:
-                weigh_part(2 * P, shared_late)
+                weigh(nc.vector, 1, 2, 0, P // 4)
             if i == 2:
-                weigh(1, 3 * P, 3 * P + P // 2)
+                weigh(nc.vector, 1, 3, 0, P // 2)
             if i == 3:
-                weigh(1, 3 * P + P // 2, R, 3 * P)
+                weigh(nc.vector, 1, 3, P // 2, P)
             quantise_h(1, i * P, (i + 1) * P)
             second_pass(i, 1)
             for cols, part in acc[i]:

from contextlib import ExitStack

import concourse.mybir as mybir
from concourse.masks import make_identity

N, C, D, R = 1024, 2048, 512, 512
FLOPS = 2 * 2 * R * N * D

F32 = mybir.dt.float32
BF16 = mybir.dt.bfloat16
I32 = mybir.dt.int32
U32 = mybir.dt.uint32
U16 = mybir.dt.uint16
U8 = mybir.dt.uint8
E4M3 = mybir.dt.float8_e4m3fn_x4
E5M2 = mybir.dt.float8_e5m2_x4
ALU = mybir.AluOpType
ACT = mybir.ActivationFunctionType

P = 128
LANES = 4
PASS = P * LANES
GROUPS = N // PASS


def tile_attend_gpq_pl_hub_x_kernel(tc, xT, cb, norm, ts, y, wt, offs, out_0, out_1, out_2):
    nc = tc.nc
    with ExitStack() as ctx:
        sb = ctx.enter_context(tc.tile_pool(name="sb", bufs=1))
        laid = ctx.enter_context(tc.tile_pool(name="laid", bufs=1))
        ps = ctx.enter_context(tc.psum_pool(name="ps", bufs=1))

        def bank(b, shape):
            return ps.tile(shape, F32, name="bank%d" % b)

        def mx_tiles(name, width, codes_tag=None):
            codes = sb.tile([P, width], U32, name=name + "_codes", tag=codes_tag or name + "_codes", align_bytes=64)
            scales = sb.tile([P, width], U8, name=name + "_scales", align_bytes=64)
            return codes, scales

        def deal(engine_copy, dst, src):
            engine_copy(dst.rearrange("p j s t -> p s t j"), src.rearrange("p t (s j) -> p s t j", j=LANES))

        norm_col = sb.tile([P, GROUPS, LANES], F32, name="norm_col")
        nc.sync.dma_start(norm_col[:], norm[0:1, :].rearrange("o (g m c) -> (o m) g c", g=GROUPS, c=LANES))
        lists = sb.tile([P, N // 16], U16, name="lists")
        nc.sync.dma_start(lists[:], offs)
        cb_planes = cb.rearrange("(p t) c -> p t c", t=LANES)
        book = [sb.tile([P, C], F32, name="book%d" % t) for t in range(LANES)]
        x_planes = xT.rearrange("(p t) r -> p t r", t=LANES)
        x_raw = [sb.tile([P, LANES, R // 2], F32, name="x_raw0", align_bytes=64),
                 laid.tile([P, LANES, R // 2], F32, name="x_raw1", align_bytes=64, offset=12288)]
        y_rows = y.rearrange("(p i) n -> p i n", i=LANES)
        y_raw = {}

        def load_y(g, i):
            if (g, i) == (0, LANES - 1):
                y_raw[g, i] = laid.tile([P, PASS], F32, name="y_raw03", align_bytes=64, offset=3072)
            else:
                y_raw[g, i] = sb.tile([P, PASS], F32, name="y_raw%d%d" % (g, i), align_bytes=64)
            nc.sync.dma_start(y_raw[g, i][:], y_rows[:, i, g * PASS:(g + 1) * PASS])

        ts_col = sb.tile([P, GROUPS, LANES], F32, name="ts_col")
        wt_col = sb.tile([P, LANES], F32, name="wt_col")
        for t in range(LANES):
            nc.sync.dma_start(book[t][:], cb_planes[:, t, :])
            if t == 0:
                nc.sync.dma_start(ts_col[:], ts[0:1, :].rearrange("o (g s j) -> (o s) g j", g=GROUPS, j=LANES))
                nc.sync.dma_start(wt_col[:], wt.rearrange("(p i) o -> p (i o)", i=LANES))
        for g in range(GROUPS):
            for i in range(LANES):
                load_y(g, i)
                if (g, i) == (0, 1):
                    for a in range(2):
                        nc.sync.dma_start(x_raw[a][:], x_planes[:, :, a * (R // 2):(a + 1) * (R // 2)])

        ident = sb.tile([P, P], F32, name="ident")
        make_identity(nc, ident[:])

        norm_all = [laid.tile([P, PASS], F32, name="norm_all0", align_bytes=64, offset=23552), sb.tile([P, PASS], F32, name="norm_all1")]
        for g in range(GROUPS):
            spread = bank(4 + g, [P, LANES, P])
            for c in range(LANES):
                nc.tensor.transpose(spread[:, c, :], norm_col[:, g, c:c + 1].to_broadcast([P, P]), ident[:])
            (nc.vector.tensor_copy, nc.scalar.copy)[g](norm_all[g][:].rearrange("p (m c) -> p m c", c=LANES), spread[:].rearrange("p c m -> p m c"))
        norm_later = sb.tile([P, PASS], F32, name="norm_later")
        nc.scalar.copy(norm_later[:], norm_all[0][:])

        wt_all = bank(7, [P, R])
        for i in range(LANES):
            nc.tensor.transpose(wt_all[:, i * P:(i + 1) * P], wt_col[:, i:i + 1].to_broadcast([P, P]), ident[:])

        wt_rows = sb.tile([P, R - P], F32, name="wt_rows")
        nc.scalar.copy(wt_rows[:], wt_all[:, P:R])

        k_f32 = {}
        for g in range(GROUPS):
            for u in range(2):
                if (g, u) == (0, 0):
                    k_f32[g, u] = laid.tile([P, 2, PASS], F32, name="k_f32_00", align_bytes=64, offset=8192)
                elif u == 1:
                    k_f32[g, u] = laid.tile([P, 2, PASS], F32, name="k_f32_%d1" % g, align_bytes=64, offset=20480 + 4096 * g)
                else:
                    k_f32[g, u] = sb.tile([P, 2, PASS], F32, name="k_f32_%d%d" % (g, u), align_bytes=64)
        k_bf = [sb.tile([P, LANES, P, LANES], BF16, name="k_bf%d" % g, align_bytes=64) for g in range(GROUPS)]

        def round_k(g, u, n0, n1):
            deal(nc.scalar.copy, k_bf[g][:, :, n0 // LANES:n1 // LANES, 2 * u:2 * u + 2], k_f32[g, u][:, :, n0:n1])

        def gather(t, g, n0, n1):
            first = g * PASS
            nc.vector.tensor_tensor(
                k_f32[g, t // 2][:, t % 2, n0:n1], book[t][:].indirect(lists[:, (first + n0) // 16:(first + n1) // 16]),
                (norm_later if g == 0 and t > 0 else norm_all[g])[:, n0:n1], ALU.mult)

        for t in range(LANES):
            if t == 1:
                picked = laid.tile([P, PASS], F32, name="picked", align_bytes=64, offset=23552)
                nc.scalar.activation(picked[:], book[t][:].indirect(lists[:, PASS // 16:N // 16]), ACT.Copy)
            for g in range(GROUPS):
                if (t, g) == (1, 1):
                    nc.vector.tensor_tensor(k_f32[g, 0][:, t, :], picked[:], norm_all[g][:], ALU.mult)
                elif (t, g) == (LANES - 1, 0):
                    gather(t, g, 0, PASS // 2)
                    gather(t, g, PASS // 2, PASS)
                else:
                    gather(t, g, 0, PASS)
                if t == 1:
                    round_k(g, 0, 0, PASS)

        ts_flat = ts_col[:].rearrange("p g j -> p (g j)")
        ts_sq = sb.tile([P, GROUPS * LANES], F32, name="ts_sq")
        nc.scalar.activation(ts_sq[:], ts_flat, ACT.Square)
        ts_hi = sb.tile([P, GROUPS * LANES], F32, name="ts_hi")
        nc.scalar.activation(ts_hi[:], ts_flat, ACT.Abs)
        ts_lo = sb.tile([P, GROUPS * LANES], F32, name="ts_lo")
        nc.scalar.activation(ts_lo[:], ts_hi[:], ACT.Copy, scale=-1.0)

        kd, kn, kn_bf, clipped, h_bf, hq, y_turned, ts_y, scores, k_turned, y_dealt = {}, {}, {}, {}, {}, {}, {}, {}, {}, {}, {}

        def quantise_k_along_d(g):
            kd[g] = (laid.tile([P, PASS], U32, name="kd%d_codes" % g, align_bytes=64, offset=12288 + 2048 * g),
                     sb.tile([P, PASS], U8, name="kd%d_scales" % g, align_bytes=64))
            nc.vector.quantize_mx(kd[g][0][:].bitcast(E4M3), kd[g][1][:], k_bf[g][:].rearrange("p j s t -> p (j s t)"))

        def turn_k(g, u, b):
            words = k_bf[g][:].rearrange("p j s t -> p (j s t)").bitcast(F32).rearrange("p (j s u) -> p j s u", j=LANES, u=2)
            k_turned[g, u] = bank(b, [P, LANES, P])
            for j in range(LANES):
                nc.tensor.transpose(k_turned[g, u][:, j, :], words[:, j, :, u], ident[:])

        def weave_k(g, u):
            if u == 0:
                kn_bf[g] = laid.tile([P, P, 2, 2, LANES], BF16, name="kn_bf%d" % g, align_bytes=64, offset=4096 * g)
            nc.scalar.copy(
                kn_bf[g][:, :, u, :, :],
                k_turned[g, u][:].rearrange("s j p -> s (j p)").bitcast(BF16).rearrange("s (j p e) -> s p e j", j=LANES, e=2))

        def quantise_k_along_n(g):
            kn[g] = mx_tiles("kn%d" % g, D, ("diff2", "ts_y7")[g])
            nc.vector.quantize_mx(kn[g][0][:].bitcast(E4M3), kn[g][1][:], kn_bf[g][:].rearrange("s p u e j -> s (p u e j)"))

        def turn_y(g, j, i):
            if i == 0:
                y_turned[g, j] = bank((0, 1, 2, 3, 2, 4, 5, 2)[g * LANES + j], [P, R])
            cols = y_dealt[g, i][:, j, :] if (g, i) in y_dealt else y_raw[g, i][:, j:PASS:LANES]
            nc.tensor.transpose(y_turned[g, j][:, i * P:(i + 1) * P], cols, ident[:])

        def deal_y(g, i):
            y_dealt[g, i] = laid.tile([P, LANES, P], F32, name="y_dealt%d" % i, align_bytes=64, offset=10240)
            nc.gpsimd.tensor_scalar(y_dealt[g, i][:].rearrange("p j (c q) -> p c j q", q=LANES),
                                    y_raw[g, i][:].rearrange("p (c q j) -> p c j q", q=LANES, j=LANES), 1.0, 0.0, ALU.mult, ALU.add)

        def scale_y(g, j):
            col = g * LANES + j
            ts_y[g, j] = sb.tile([P, R], F32, name="ts_y%d" % col, align_bytes=64)[:]
            nc.scalar.activation(ts_y[g, j], y_turned[g, j][:], ACT.Copy, scale=ts_flat[:, col:col + 1])

        def score(g, j):
            col = g * LANES + j
            scores[g, j] = bank((6, 0, 1, 2, 3, 6, 0, 1)[col], [P, R])
            cols = slice(j * P, (j + 1) * P)
            nc.tensor.matmul_mx(scores[g, j][:], kd[g][0][:, cols].bitcast(E4M3), kd[g][1][:, cols],
                                x_codes[:].bitcast(E4M3), x_scales[:], start=True, stop=True)

        def residual(g, j):
            col = g * LANES + j
            tag = "diff%d" % col
            diff = sb.tile([P, R], F32, name="diff%d" % col, tag=tag, align_bytes=64)[:]
            nc.vector.scalar_tensor_tensor(diff, scores[g, j][:], ts_sq[:, col:col + 1], ts_y[g, j], ALU.mult, ALU.subtract)
            return diff

        def clip(g, j, diff):
            col = g * LANES + j
            engine = nc.vector if j >= 2 else nc.gpsimd
            pieces = (slice(0, R // 2), slice(R // 2, R)) if j == LANES - 1 else (slice(0, R),)
            for rows in pieces:
                engine.tensor_scalar(clipped[g][:, j, rows], diff[:, rows], ts_hi[:, col:col + 1], ts_lo[:, col:col + 1],
                                     ALU.min, ALU.max)

        def weigh(engine, g, i, m0, m1):
            r0, r1 = i * P + m0, i * P + m1
            factors = wt_rows[:, r0 - P:r1 - P] if engine is nc.gpsimd else wt_all[:, r0:r1]
            engine.tensor_tensor(
                h_bf[g, i * P][:, m0:m1, :].rearrange("s (c q) j -> s c j q", q=2),
                clipped[g][:, :, r0:r1].rearrange("s j (c q) -> s c j q", q=2),
                factors.rearrange("s (c q) -> s c q", q=2).unsqueeze(2).to_broadcast([P, (m1 - m0) // 2, LANES, 2]),
                ALU.mult)

        def h_tile(g, i, offset=None):
            if offset is None:
                h_bf[g, i * P] = sb.tile([P, P, LANES], BF16, name="h_bf%d_%d" % (g, i), align_bytes=64)
            else:
                h_bf[g, i * P] = laid.tile([P, P, LANES], BF16, name="h_bf%d_%d" % (g, i), align_bytes=64, offset=offset)

        def weigh_turned(g, i, b, b_back, first):
            turned = bank(b, [P, LANES, P])
            for j in range(LANES):
                nc.tensor.transpose(turned[:, j, :], clipped[g][:, j, i * P:(i + 1) * P], ident[:])
            by_row = sb.tile([P, 2, P, 2], BF16, name="by_row%d" % g, align_bytes=64)
            nc.scalar.activation(by_row[:], turned[:].rearrange("m (v e) s -> m v s e", e=2), ACT.Copy, scale=wt_col[:, i:i + 1])
            words = by_row[:].rearrange("m v s e -> m (v s e)").bitcast(F32)

            def turn_back():
                back = bank(b_back, [P, 2, P])
                for v in range(2):
                    nc.tensor.transpose(back[:, v, :], words[:, v * P:(v + 1) * P], ident[:])
                rows = h_bf[g, first][:, i * P - first:(i + 1) * P - first, :].rearrange("s m j -> s (m j)").bitcast(F32)
                nc.scalar.copy(rows.rearrange("s (m v) -> s m v", v=2), back[:].rearrange("s v m -> s m v"))
            return turn_back

        def quantise_h(g, r0, r1, codes_tag=None):
            codes, scales = mx_tiles("h%d_%d" % (g, r0), r1 - r0, codes_tag)
            nc.vector.quantize_mx(codes[:].bitcast(E5M2), scales[:], h_bf[g, r0][:].rearrange("s r j -> s (r j)"))
            for first in range(r0, r1, P):
                cols = slice(first - r0, first - r0 + P)
                hq[g, first // P] = codes[:, cols], scales[:, cols]

        for g in range(GROUPS):
            clipped[g] = sb.tile([P, LANES, R], F32, name="clipped%d" % g)

        x_bf = laid.tile([P, LANES, P, LANES], BF16, name="x_bf", align_bytes=64, offset=8192)
        x_codes, x_scales = mx_tiles("x", R)
        turn_k(0, 0, 4)
        round_k(0, 1, 0, PASS // 2)
        round_k(0, 1, PASS // 2, PASS)
        round_k(1, 1, 0, PASS)
        turn_k(0, 1, 5)
        for a in range(2):
            deal(nc.vector.tensor_copy, x_bf[:, :, a * (P // 2):(a + 1) * (P // 2), :], x_raw[a][:])
        quantise_k_along_d(0)
        nc.vector.quantize_mx(x_codes[:].bitcast(E4M3), x_scales[:], x_bf[:].rearrange("p i m t -> p (i m t)"))
        quantise_k_along_d(1)
        deal_y(1, 0)
        for i in range(LANES):
            for j in range(LANES):
                turn_y(0, j, i)
        for j in range(LANES):
            scale_y(0, j)
        diffs = {}
        for j in range(LANES):
            score(0, j)
            diffs[0, j] = residual(0, j)
        for j in range(LANES):
            clip(0, j, diffs[0, j])
        weave_k(0, 0)
        weave_k(0, 1)
        for j in range(LANES):
            score(1, j)
        for j in range(LANES):
            for i in range(LANES):
                turn_y(1, j, i)
            scale_y(1, j)
        for u in range(2):
            turn_k(1, u, 4 + u)
            weave_k(1, u)
        for i in (0, 2, 3):
            h_tile(0, i)
        weigh(nc.vector, 0, 0, 0, P)
        weigh(nc.vector, 0, 3, 0, P // 2)
        weigh(nc.gpsimd, 0, 3, P // 2, P)
        quantise_h(0, 0, P)
        quantise_k_along_n(0)
        quantise_h(0, R - P, R)
        h_tile(0, 1, 0)
        weigh(nc.gpsimd, 0, 1, P // 4, P)
        weigh(nc.vector, 0, 1, 0, P // 4)
        for j in range(LANES):
            diffs[1, j] = residual(1, j)
        for j in range(LANES):
            clip(1, j, diffs[1, j])
        weigh_turned(0, 2, 4, 5, R // 2)()

        grad = [sb.tile([P, 2, D], F32, name="grad%d" % u) for u in range(2)]
        out_rows = out_0.rearrange("(p i) d -> p i d", i=LANES)
        acc = {}
        half = D // 2

        def second_pass(i, g):
            for cols, part in acc[i]:
                nc.tensor.matmul_mx(part[:], hq[g, i][0].bitcast(E5M2), hq[g, i][1],
                                    kn[g][0][:, cols].bitcast(E4M3), kn[g][1][:, cols], start=(g == 0), stop=(g == GROUPS - 1))

        def round_grad(engine_copy, u, cols):
            engine_copy(
                grad_bf[:, cols, 2 * u:2 * u + 2].rearrange("p (c q) i -> p c i q", q=2),
                grad[u][:, :, cols].rearrange("p i (c q) -> p c i q", q=2))

        def open_sum(i):
            if i == LANES - 1:
                acc[i] = [(slice(hh * half, (hh + 1) * half), bank(1 + hh, [P, half])) for hh in range(2)]
            else:
                acc[i] = [(slice(0, D), bank((0, 4, 6)[i], [P, D]))]
            second_pass(i, 0)

        open_sum(0)
        open_sum(3)
        for i in range(3):
            h_tile(1, i)
        weigh(nc.gpsimd, 1, 2, P // 4, P)
        weigh(nc.vector, 1, 0, 0, P)
        weigh(nc.vector, 1, 1, 0, P)
        quantise_h(0, P, 2 * P)
        open_sum(1)
        quantise_k_along_n(1)
        h_tile(1, 3, 4096)
        for i in range(LANES):
            if i == 2:
                quantise_h(0, R // 2, R - P)
                open_sum(2)
            if i == 1:
                weigh(nc.vector, 1, 2, 0, P // 4)
            if i == 2:
                weigh(nc.vector, 1, 3, 0, P // 2)
            if i == 3:
                weigh(nc.vector, 1, 3, P // 2, P)
            quantise_h(1, i * P, (i + 1) * P)
            second_pass(i, 1)
            for cols, part in acc[i]:
                nc.scalar.copy(grad[i // 2][:, i % 2, cols], part[:])
            nc.sync.dma_start(out_rows[:, i, :], grad[i // 2][:, i % 2, :])

        grad_bf = laid.tile([P, D, LANES], BF16, name="grad_bf", align_bytes=64, offset=4096)
        g_codes, g_scales = mx_tiles("grad", D)
        words_out = out_1.rearrange("o p d b -> (o p) (d b)").bitcast(I32)
        round_grad(nc.vector.tensor_copy, 0, slice(0, D))
        round_grad(nc.vector.tensor_copy, 1, slice(0, half))
        round_grad(nc.vector.tensor_copy, 1, slice(half, D))
        for hh in range(2):
            cols = slice(hh * half, (hh + 1) * half)
            nc.vector.quantize_mx(g_codes[:, cols].bitcast(E4M3), g_scales[:, cols],
                                  grad_bf[:, cols, :].rearrange("p d i -> p (d i)"))
            nc.sync.dma_start(words_out[:, cols], g_codes[:, cols].bitcast(I32))
        scales_out = out_2.rearrange("o f d -> (o f) d").bitcast(I32)
        for q in range(4):
            queue = (nc.sync, nc.scalar)[q % 2]
            queue.dma_start(scales_out[4 * q:4 * q + 4, :], g_scales[32 * q:32 * q + 4, :].bitcast(I32))
